import numpy as np, ml_dtypes
CORES = [51,54,179,182]
N = 4
BF = ml_dtypes.bfloat16
def gentries(a):
    return np.ascontiguousarray(a.reshape(8, 16, -1).transpose(0, 2, 1)).reshape(8, -1)
def gtable(e):
    e = np.asarray(e); return np.ascontiguousarray(e.reshape(8, -1, 16).transpose(0, 2, 1)).reshape(128, -1).astype(np.int32)
W, WC, FR, X, H, V, FO = 3072, 2048, 3, 768, 3, 6, 6
def loud(rng, lo, hi):
    v = 0.25 + 0.75 * rng.random((N, 8, 16, W), dtype=np.float32)
    return v * np.exp2(rng.integers(lo, hi + 1, (N, 8, 1, W)))
def perms(rng):
    return np.argsort(rng.random((N, 8, FR, W)), axis=-1)
def recs(rng):
    return 0.75 + 0.5 * rng.random((N, 8, 16, WC))
def turns(rng):
    return rng.integers(0, WC, (N, 8, W)), rng.integers(0, 4096, (N, 8, FR))
def put(a, m, v):
    i = int(np.argmax(a == v)); a[i] = a[m]; a[m] = v
def saw():
    n = np.arange(W)[None, :]; top = (16 - np.arange(16)[:, None]) % 16
    return 1.0 - np.where(n < top, top - n, (n - top) % 16) * 0.03125
def spikes(rng):
    v = 0.3125 + 0.5 * rng.random((N, 8, 16, W))
    n = rng.choice(np.array([0, 1, V - 1, V - 1, V, V, V + 1, 15, 16]), (N, 8, 1, W // 8))
    a = np.argsort(rng.random((N, 8, 16, W // 8)), axis=2) < n; k = rng.integers(0, 4, a.shape); miss = ~a & (k == 3)
    v[..., ::8] = np.where(a | miss, 1.0, 0.25)
    v[..., H::8] = np.where(miss, 1.0078125, np.where(a & (k == 1), 1.0, v[..., H::8]))
    v[..., H + 1::8] = np.where(a & (k == 2), 1.0078125, v[..., H + 1::8])
    return v
RATES = np.concatenate([np.arange(192, 256), np.arange(256, 321, 2)])
def near(k):
    s = np.concatenate([np.arange(128, 256), np.arange(256, 512, 2), np.arange(512, 1024, 4)]).astype(np.int64)
    a = np.tile(np.arange(RATES.size), s.size); s = np.repeat(s, RATES.size)
    x = s * RATES[a].astype(np.int64) ** k; b = x.astype(np.float32).view(np.int32)
    o = np.argsort(x, kind="stable"); i, j = o[:-1], o[1:]
    low = (b[i] != b[j]) & ((b[i] >> 2) == (b[j] >> 2)); tie = (x[i] != x[j]) & (b[i] == b[j])
    return s, a, [np.stack([i[w], j[w]], axis=1) for w in (low, tie) if np.any(w)]
def plant(rng, found, S, C, P, R, q, g):
    s, a, L = found; h = (W - (FR - 1) * X) // 8; n = 8 * np.arange(h)
    v = (1.0 + 0.5 * rng.random((16, 8 * h))) * 0.0625
    e = np.stack([L[int(w)][int(rng.integers(0, len(L[int(w)])))] for w in rng.integers(0, len(L), h)])
    e = np.where(rng.random((h, 1)) < 0.5, e, e[:, ::-1])
    on = np.argsort(rng.random((16, h)), axis=0) < rng.choice(np.array([V, V, 16]), h)
    for i in range(2):
        v[:, n + 3 + i] = np.where(on, s[e[:, i]] * 2.0 ** -8, v[:, n + 3 + i]); R[q, g, n + 3 + i] = a[e[:, i]]
    S[q, g, :, :8 * h] = v; C[q, g, :, :RATES.size] = RATES * 0.00390625; P[q, g, :FR - 1] = np.arange(W)
def pack(S, C, P, R, hp):
    return {"sp": np.ascontiguousarray(S.reshape(N, 128, W)).astype(BF), "rec": np.ascontiguousarray(C.reshape(N, 128, WC)).astype(BF), "itg": np.stack([gtable(a.reshape(8, FR * W)) for a in P]),
            "rot": np.ascontiguousarray(R).astype(np.int32), "hop": np.ascontiguousarray(hp).astype(np.int32)}
def setup_inputs(rng):
    S = loud(rng, -1, 1); C = recs(rng); P = perms(rng); R, hp = turns(rng)
    return pack(S, C, P, R, hp)
def setup_inputs_spread(rng):
    S = loud(rng, 0, 0) * rng.choice(np.array([0.5, 2.0]), (N, 8, 1, W)); C = recs(rng); P = perms(rng)
    R = np.exp2(np.log2(WC) * rng.random((N, 8, W))).astype(np.int64) - 1; R = np.where(rng.random(R.shape) < 0.5, R, WC - 1 - R)
    hp = np.exp2(12 * rng.random((N, 8, FR))).astype(np.int64) - 1
    found = near(FR - 1)
    for q in range(N):
        for g in range(8):
            if (q + g) % 4 == 1: plant(rng, found, S, C, P, R, q, g)
    return pack(S, C, P, np.clip(R, 0, WC - 1), np.clip(hp, 0, 4095))
def setup_inputs_ends(rng):
    share = rng.choice(np.array([0.0, 0.75, 1.0, 1.0]), (N, 8, 1, W)); share[..., 0] = 1.0; share[..., W - 1] = 1.0
    S = np.where(rng.random((N, 8, 16, W)) < share, 4.0, 0.0625)
    C = np.where(rng.random((N, 8, 16, WC)) < 0.5, 0.75, 1.25); C[..., 0] = 0.75; C[..., WC - 1] = 1.25
    P = perms(rng); R = rng.integers(0, 2, (N, 8, W)) * (WC - 1); hp = rng.integers(0, 2, (N, 8, FR)) * 4095
    hp[:, 1, 0] = 0; hp[:, 2, 0] = 4095
    for q in range(N):
        for g in range(8):
            k = (q + g) % 4
            if (q, g) in ((0, 0), (N - 1, 7)): k = 0; hp[q, g, 0] = 4095; R[q, g, 0] = WC - 1; R[q, g, W - 1] = 0
            if k == 0: P[q, g] = np.arange(W)[::-1]
            elif k == 2: P[q, g, ::2] = np.arange(W)
            else:
                for t in range(FR): put(P[q, g, t], 0, W - 1); put(P[q, g, t], W - 1, 0)
    return pack(S, C, P, R, hp)
def setup_inputs_corners(rng):
    S = loud(rng, -1, 1); C = recs(rng); P = perms(rng); R, hp = turns(rng); sk = spikes(rng); teeth = saw()
    for q in range(N):
        for g in range(8):
            k = (q + g) % 8
            if k == 0: S[q, g] = 0.75
            elif k == 1:
                S[q, g] = teeth; C[q, g] = 1.0
                for t in range(FR): put(P[q, g, t], (W - 1, 0, W // 2, W - 1)[q % 4], 0)
            elif k == 2: S[q, g] = sk[q, g]; P[q, g] = np.arange(W)
            elif k == 3: S[q, g] = sk[q, g]; P[q, g] = np.arange(W)[::-1]
            elif k == 4: S[q, g] = np.where(np.repeat(rng.random(W // 64) < 0.6, 64), S[q, g], 0.0625)
            elif k == 5: P[q, g] = (np.arange(W) + 1) % W
            elif k == 6:
                v = teeth.copy(); v[:, W - 1] = 1.5; S[q, g] = v
                for t in range(FR): put(P[q, g, t], 100, W - 1); put(P[q, g, t], 300, 0)
            else: R[q, g] = rng.integers(0, 2, W) * (WC - 1); hp[q, g] = rng.integers(0, 2, FR) * 4095
    for q, place in ((1, 0), (3, W - 1)):
        for a, g in ((q - 1, 5), (q - 1, 6), (q - 1, 7), (q, 7)):
            S[a, g] = teeth; P[a, g] = perms(rng)[a, g]; P[a, g, :FR - 1] = np.arange(W); R[a, g] = rng.integers(0, 4, W)
            C[a, g] = 0.75 + 0.5 * rng.random((16, WC)); C[a, g, :, :4] = 1.0
        put(P[q, 7, FR - 1], place, 0); hp[q, 7, FR - 1] = 4095
    return pack(S, C, P, R, hp)
def setup_inputs_crowd(rng):
    S = np.zeros((N, 8, 16, W)); C = recs(rng); P = perms(rng); R, hp = turns(rng); teeth = saw(); flat = (16, 15, V + 1, V, V - 1, V - 2, 1, 0)
    for q in range(N):
        for g in range(8):
            v = teeth.copy(); v[rng.permutation(16)[:flat[(q + g) % 8]]] = 0.75; S[q, g] = v * 0.125
    C[::2] = 0.75 + 0.0078125 * rng.integers(0, 65, C[::2].shape[:3] + (1,))
    return pack(S, C, P, R, hp)
def setup_inputs_calm(rng):
    S = spikes(rng) * 0.25; C = recs(rng); C[::2] = 1.0; R, hp = turns(rng); hp[:] = 0
    few = rng.choice(np.array([0, 1, 2, 3, 8, W - 1, W - 8]), (N, 8, FR, 1)); P = (np.arange(W) + few) % W
    R = np.where(np.arange(8)[None, :, None] % 2 == 0, rng.integers(0, 4, R.shape), rng.integers(WC - 2, WC, R.shape))
    C[1::2, :, :, [0, 1, 2, 3, WC - 2, WC - 1]] = np.array([0.75, 0.875, 1.0, 1.125, 1.25, 0.8125])
    return pack(S, C, P, R, hp)
def check_ranges(d):
    bad = []
    for k, lo, hi in (("itg", 0, W - 1), ("rot", 0, WC - 1), ("hop", 0, 4095)):
        if np.min(d[k]) < lo or np.max(d[k]) > hi: bad.append("range of " + k)
    p = np.sort(np.stack([gentries(a) for a in d["itg"]]).reshape(N, 8, FR, W), axis=-1)
    if not np.all(p == np.arange(W)): bad.append("itg: no permutation")
    s = np.asarray(d["sp"]).astype(np.float64); c = np.asarray(d["rec"]).astype(np.float64)
    if not np.all((s >= 0.0625) & (s <= 4)): bad.append("range of sp")
    if not np.all((c >= 0.75) & (c <= 1.25)): bad.append("range of rec")
    return bad
def reference(sp, rec, itg, rot, hop):
    S = sp.astype(np.float32).reshape(N, 8, 16, W); C = rec.astype(np.float32).reshape(N, 8, 16, WC); R = rot.astype(np.int64); hp = hop.astype(np.int64)
    P = np.stack([gentries(a) for a in itg]).astype(np.int64).reshape(N, 8, FR, W); m = np.arange(W)
    for t in range(FR):
        vote = np.ones(S.shape, bool)
        for d in range(1, H + 1):
            vote[..., d:] &= S[..., d:] >= S[..., :-d]; vote[..., :-d] &= S[..., :-d] >= S[..., d:]
        peak = np.add.reduce(vote, axis=2, dtype=np.int64) >= V; peak[..., 0] = True
        it = P[:, :, t]; moved = np.take_along_axis(peak, it, 2)
        left = np.maximum.accumulate(np.where(moved, m, -2 * W), axis=-1)
        right = np.minimum.accumulate(np.where(moved, m, 3 * W)[..., ::-1], axis=-1)[..., ::-1]
        q = np.where(m - left <= right - m, left, right); p = np.take_along_axis(it, q, 2)
        src = np.clip(p + m - q, 0, W - 1)
        T = np.take_along_axis(S, src[:, :, None, :], 3)
        Q = (np.take_along_axis(R, src, 2) + hp[:, :, t, None] * (q - p)) & (WC - 1)
        T = np.concatenate([np.roll(T[..., W - X:], (1, t), axis=(0, 1)), T[..., :W - X]], axis=-1)
        R = np.concatenate([np.roll(Q[..., W - X:], (1, t), axis=(0, 1)), Q[..., :W - X]], axis=-1)
        S = T * np.take_along_axis(C, R[:, :, None, :], 3)
    y = np.add.reduce(S.astype(np.float64).reshape(N, 128, FO, W // FO), axis=2)
    return {"y": y.astype(np.float32)}

def check_inputs(d):
    bad = list(check_ranges(d))
    if not bad:
        for name, y in reference(**d).items():
            for q in range(N):
                v = np.abs(np.asarray(y[q], np.float64)); s = np.sqrt(np.mean(v * v))
                if v.max() > 7 * s or s < 2.0 ** -3: bad.append('%s of rank %d is uneven or too small' % (name, q))
    return bad

@@ -1,0 +1,543 @@
+from concourse.mybir import AluOpType as A, ActivationFunctionType as F
+
+W, WC, FR, X = 3072, 2048, 3, 768
+HUGE = float(2 ** 26)
+BIG = 2 ** 23
+C0 = -(2 ** 24) + 2 ** 18
+VS, VB = 64.0, -22.0
+FP, BP = 8, 16
+
+K1, K2, CQ, PE, W0, W1, RE, FO = 48, 96, "v", 3, 0, 4, 1, 0
+K3, W2 = 120, 12
+
+f32, bf, i32, u16 = "float32", "bfloat16", "int32", "uint16"
+SCRATCH = {
+    "Sb": ("sbuf", [128, W + 2 * BP], bf), "S1": ("sbuf", [128, W + 2 * FP], f32), "S2": ("sbuf", [128, W + 2 * FP], f32),
+    "T0": ("sbuf", [128, W], bf), "T1": ("sbuf", [128, W], f32), "T2": ("sbuf", [128, X], f32),
+    "Ts0": ("sbuf", [128, X], bf), "Ts1": ("sbuf", [128, X], f32), "Ts2": ("sbuf", [128, X], f32),
+    "L0": ("dram", [1, 128, X], bf), "L1": ("dram", [2, 128, X // 2], f32),
+    "Qu0": ("sbuf", [128, 192], u16), "Qu1": ("sbuf", [128, 192], u16), "Qu2": ("sbuf", [128, 192], u16),
+    "Qs": ("sbuf", [128, 144], u16),
+    "C2": ("sbuf", [128, 2 * WC], bf), "Rw": ("sbuf", [128, W], bf), "Rg": ("sbuf", [128, W], bf),
+    "V": ("sbuf", [128, W], bf), "G": ("sbuf", [128, 2 * 98 * 16], bf),
+    "Hf": ("sbuf", [128, 3080], f32), "Gb": ("sbuf", [128, 3080], bf), "Hb": ("sbuf", [128, 3080], bf), "msk": ("sbuf", [128, 945], bf),
+    "iti": ("sbuf", [128, 576], i32), "Lit": ("sbuf", [128, 2, 288], u16), "itf": ("sbuf", [128, 2, 290], f32),
+    "roti": ("sbuf", [128, 192], i32), "hpi": ("sbuf", [128, 4], i32), "hpf": ("sbuf", [128, 4], f32),
+    "g8": ("sbuf", [128, 2], f32), "hv": ("sbuf", [128, 8], f32),
+    "Rhi": ("sbuf", [128, 192], bf), "Rlo": ("sbuf", [128, 192], bf), "Rge": ("sbuf", [128, 192], bf), "Qf": ("sbuf", [128, 192], f32),
+    "KF": ("sbuf", [128, 512], f32), "KB": ("sbuf", [128, 512], f32),
+    "LF": ("sbuf", [128, 512], f32), "LB": ("sbuf", [128, 512], f32),
+    "MF": ("sbuf", [128, 256], f32), "MB": ("sbuf", [128, 256], f32),
+    "Lf": ("sbuf", [128, 16], f32), "Lm": ("sbuf", [128, 16], u16),
+    "B2": ("sbuf", [128, 192], f32), "Wi": ("sbuf", [128, 192], i32), "Dd": ("sbuf", [128, 192], f32),
+    "pi": ("sbuf", [128, 192], i32), "di": ("sbuf", [128, 192], i32), "Ls": ("sbuf", [128, 192], u16),
+    "dm": ("sbuf", [128, 192], f32), "ei": ("sbuf", [128, 192], i32), "em": ("sbuf", [128, 192], i32), "ef": ("sbuf", [128, 192], f32),
+    "c17": ("sbuf", [128, 192], f32), "mc": ("sbuf", [128, 192], f32),
+    "of": ("sbuf", [128, 256], f32), "ob": ("sbuf", [128, 96], bf), "o8": ("sbuf", [128, 8], bf), "nb": ("sbuf", [128, 8], bf),
+    "Iw": ("sbuf", [128, 160], f32), "I97": ("sbuf", [128, 96], f32), "Ew": ("sbuf", [128, 256], f32),
+    "ind": ("sbuf", [128, 8], bf), "tm8": ("sbuf", [128, 8], bf), "tn8": ("sbuf", [128, 8], bf),
+    "Z": ("sbuf", [128, 176], bf), "Rr": ("sbuf", [128, W], bf), "crow": ("sbuf", [128, 2, 512], bf),
+    "Wb0": ("sbuf", [128, 784], bf), "Wb1": ("sbuf", [128, 784], bf), "Wf0": ("sbuf", [128, 944], f32), "Wf1": ("sbuf", [128, 944], f32),
+    "Ib": ("sbuf", [128, 128], bf), "Jb": ("sbuf", [128, 128], bf), "Jf": ("sbuf", [128, 128], f32),
+    "Y": ("sbuf", [128, 512], f32),
+    "PA": ("psum", [128, 1024], f32), "PB": ("psum", [128, 1024], f32), "D": ("psum", [128, 512], f32),
+    "X0": ("psum", [128, 512], f32), "X1": ("psum", [128, 512], f32), "X2": ("psum", [128, 8, 64], f32),
+}
+SEMAPHORES = ["qv", "qs", "qt", "qg", "sent", "sp0", "sp1", "sp2", "sp3", "rec", "itg", "rot", "hop", "rw", "rw0", "rw1",
+              "aT00", "aT10", "aT11", "aT20", "aT21", "aQ0", "aQ1", "aQ2", "lT00", "lT10", "lT11", "y0", "y1"]
+
+
+def rev(lo, hi):
+    return slice(hi - 1, lo - 1 if lo > 0 else None, -1)
+
+
+def meets(a, b):
+    return a[0] == b[0] and a[1] < b[2] and b[1] < a[2]
+
+
+def tok(x):
+    return (x, 0, 1 << 30) if isinstance(x, str) else x
+
+
+def emit(g, T, ops):
+    eng = {"v": g.vector, "s": g.scalar, "t": g.tensor, "g": g, "y": g.sync}
+    known = {q: {} for q in eng}
+    pos = {q: 0 for q in eng}
+    needed = set()
+    for i, o in enumerate(ops):
+        q = o["q"]
+        if o["sem"] is None:
+            o["src"], o["pos"] = q, pos[q]
+            pos[q] += 1
+        else:
+            o["src"], o["pos"] = "d" + o["sem"], 0
+        o["waits"] = []
+        if q is None:
+            o["known"] = {}
+            continue
+        deps = {}
+        for j in range(i):
+            p = ops[j]
+            same = p["q"] == q and p["sem"] is None and o["sem"] is None
+            if same and q == "t":
+                continue
+            hit = any(meets(a, b) for a in p["W"] for b in o["R"] + o["W"]) or any(meets(a, b) for a in p["R"] for b in o["W"])
+            if not hit and p["q"] != q:
+                hit = any(b in p["X"] for b in o["X"])
+            if hit and (p["src"] not in deps or ops[deps[p["src"]]]["pos"] < p["pos"]):
+                deps[p["src"]] = j
+        for j in sorted(deps.values(), reverse=True):
+            p = ops[j]
+            if known[q].get(p["src"], -1) >= p["pos"]:
+                continue
+            o["waits"].append(j)
+            needed.add(j)
+            for s, n in p["known"].items():
+                known[q][s] = max(known[q].get(s, -1), n)
+            known[q][p["src"]] = max(known[q].get(p["src"], -1), p["pos"])
+        o["known"] = dict(known[q])
+    count = {q: 0 for q in eng}
+    for i, o in enumerate(ops):
+        q = o["q"]
+        if o["sem"] is None and i in needed:
+            count[q] += 1
+            o["val"] = ("q" + q, count[q])
+        elif o["sem"] is not None:
+            o["val"] = (o["sem"], o["n"])
+        if q is None:
+            continue
+        for j in o["waits"]:
+            s, n = ops[j]["val"]
+            eng[q].wait_ge(T.sem[s], n)
+        r = o["fn"](eng[q])
+        if o["sem"] is not None:
+            for x in r:
+                x.then_inc(T.sem[o["sem"]], 16)
+        elif i in needed:
+            r.then_inc(T.sem["q" + q], 1)
+
+
+def rank_program(g, core, T, topo):
+    rank = T.rank_of(core)
+    if rank is None:
+        return
+    N = len(T.cores)
+    nxt, prv = T.cores[(rank + 1) % N], T.cores[(rank - 1) % N]
+    rid, pid = topo.addr(nxt, core)
+    out_mask, n_out, n_in = topo.mask(core, nxt), len(topo.engines(core, nxt)), len(topo.engines(prv, core))
+    ops = []
+    sends = [0]
+
+    def op(q, fn, R=(), Wr=(), Xb=(), sem=None, n=0):
+        ops.append({"q": q, "fn": fn, "R": [tok(x) for x in R], "W": [tok(x) for x in Wr], "X": list(Xb), "sem": sem, "n": n})
+
+    def turned(shift):
+        if shift == 0:
+            return [(slice(0, 128), slice(0, 128))]
+        return [(slice(0, 128 - shift), slice(shift, 128)), (slice(128 - shift, 128), slice(0, shift))]
+
+    def dmas(q, sem, pairs, R, Wr):
+        op(q, lambda e: [e.dma_start(a, b) for a, b in pairs], R, Wr, sem=sem, n=16 * len(pairs))
+
+    def send(dst, src, sem, R):
+        sends[0] += n_out
+        op("g", lambda e: e.remote_dma(dst, src, T.sem[sem], T.sem.sent, pid, rid, out_mask), R)
+
+    def arrive(sem, Wr):
+        op(None, None, (), Wr, sem=sem, n=n_in)
+
+    def vmem(ap, val, Wr):
+        op("v", lambda e: e.memset(ap, val), (), Wr)
+
+    def vcopy(o, i, R, Wr, Xb=()):
+        op("v", lambda e: e.tensor_copy(o, i), R, Wr, Xb)
+
+    def vtt(o, a, b, alu, R, Wr, Xb=()):
+        op("v", lambda e: e.tensor_tensor(o, a, b, alu), R, Wr, Xb)
+
+    def vts(o, a, s1, s2, o0, o1, R, Wr, Xb=()):
+        if s2 is None:
+            op("v", lambda e: e.tensor_scalar(o, a, s1, None, o0), R, Wr, Xb)
+        else:
+            op("v", lambda e: e.tensor_scalar(o, a, s1, s2, o0, o1), R, Wr, Xb)
+
+    def vscan(o, a, b, init, o0, o1, R, Wr, Xb=()):
+        op("v", lambda e: e.tensor_tensor_scan(o, a, b, init, o0, o1), R, Wr, Xb)
+
+    def acopy(o, i, R, Wr, Xb=()):
+        op("s", lambda e: e.activation(o, i, F.Copy), R, Wr, Xb)
+
+    def mm(lst, R, Wr, Xb):
+        def fn(e):
+            r = None
+            for a in lst:
+                r = e.matmul(*a)
+            return r
+        op("t", fn, R, Wr, Xb)
+
+    def iota(o, pat, base, cm, Wr, high=False):
+        op("g", lambda e: e.iota(o, pat, base, cm, allow_small_or_imprecise_dtypes=True), [] if high else ["pool"], Wr + (["pool"] if high else []))
+
+    def sel(o, i, pat, cmp, base, cm, R, Wr):
+        op("g", lambda e: e.affine_select(o, i, pat, cmp, 0.0, base, cm), R + ["pool"], Wr)
+
+    XB = {"X0": 5, "X1": 6, "X2": 7}
+    sh = (32 * rank) % 128
+    lay = turned(sh)
+
+    cuts = [0, 768, 1544, 2312, W]
+    for c in range(4):
+        a, b = cuts[c], cuts[c + 1]
+        dmas("y", "sp%d" % c, [(T.Sb[p, BP + a:BP + b], T.sp[r, a:b]) for p, r in lay], (), [("Sb", 3 + a, 3 + b)])
+    dmas("s", "hop", [(T.hpi[0:8, 0:3], T.hop[:, :])], (), ["hpi"])
+    dmas("s", "rot", [(T.roti[p, :], T.rot[r.start // 16:r.stop // 16, :]) for p, r in lay], (), ["roti"])
+    dmas("s", "itg", [(T.iti[p, :], T.itg[r, :]) for p, r in lay], (), ["iti"])
+    dmas("y", "rec", [(T.C2[p, k * WC:(k + 1) * WC], T.rec[r, :]) for k in range(2) for p, r in lay], (), ["C2"])
+
+    vmem(T.of[:, :], 1.0, ["of"])
+    vmem(T.msk[:, :], 1.0, ["msk"])
+    vmem(T.Sb[:, 0:BP], 0.0, [("Sb", 0, 3)])
+    vmem(T.Sb[:, BP + W:], 0.0, [("Sb", 3 + W, 4000)])
+    vmem(T.msk[:, 0:945:7], 0.0, ["msk"])
+    vmem(T.o8[:, :], 1.0, ["o8"])
+    vmem(T.Z[:, :], 0.0, ["Z"])
+    vmem(T.V[:, 0:1], 1.0, [("V", 0, 1)])
+    for u in range(2):
+        vmem(T.G[:, 1568 * u:1568 * u + 16], -1.0, [("G", 10 + 2 * u, 11 + 2 * u)])
+        vmem(T.G[:, 1568 * u + 1552:1568 * u + 1568], -1.0, [("G", 11 + 2 * u, 12 + 2 * u)])
+    vmem(T.c17[:, :], float(2 ** 17), ["c17"])
+
+    def fill(o, n, val, Wr):
+        iota(o, [[0, n]], val, 0, Wr)
+
+    def zero(nm, which):
+        for c in which:
+            op("s", lambda e, a=X * c: e.activation(T[nm][:, a:a + X], T.msk[:, 0:X], F.Copy, scale=0.0), ["msk"], [(nm, 4 * c, 4 * c + 4)])
+
+    sel(T.Iw[:, 0:128], T.of[:, 0:128], [[1, 128]], A.is_equal, 0, -1, ["of"], [("Iw", 0, 1)])
+    acopy(T.Ib[:, :], T.Iw[:, 0:128], [("Iw", 0, 1)], ["Ib"])
+    op("s", lambda e: e.activation(T.Jb[:, :], T.Iw[:, 0:128], F.Copy, scale=-1.0), [("Iw", 0, 1)], ["Jb"])
+    op("s", lambda e: e.activation(T.Jf[:, :], T.Iw[:, 0:128], F.Copy, scale=-1.0), [("Iw", 0, 1)], ["Jf"])
+    zero("Rw", range(4))
+    zero("Rr", range(2))
+    iota(T.crow[0:1, 0, :], [[0, 8], [-1, 64]], 16, 0, [("crow", 0, 1)])
+    fill(T.ob[0:1, :], 96, 8192, ["ob"])
+    iota(T.itf[:, :, 0:290:289], [[0, 2], [0, 2]], 0, 0, [("itf", 0, 1), ("itf", 289, 290)])
+    iota(T.itf[:, :, 97:194:96], [[0, 2], [0, 2]], 0, 0, [("itf", 97, 98), ("itf", 193, 194)])
+    fill(T.crow[0:1, 0, 0:512:64], 8, int(HUGE) // 8192, [("crow", 0, 1)])
+    iota(T.crow[0:1, 1, :], [[0, 8], [1, 64]], -16, 0, [("crow", 1, 2)])
+    fill(T.crow[0:1, 1, 63:512:64], 8, int(HUGE) // 8192, [("crow", 1, 2)])
+    sel(T.Ew[0:8, :], T.of[0:8, :], [[0, 2], [1, 128]], A.is_ge, 0, -16, ["of"], ["Ew"])
+    iota(T.g8[0:8, :], [[0, 2]], 0, 16, ["g8"])
+    sel(T.Ew[0:8, :], T.Ew[0:8, :], [[0, 2], [-1, 128]], A.is_ge, 15, 16, ["Ew"], ["Ew"])
+    iota(T.Lf[:, :], [[16, 2], [64, 8]], 0, 1, ["Lf"])
+    sel(T.Iw[:, 128:160], T.of[:, 0:32], [[1, 32]], A.is_equal, 0, -1, ["of"], [("Iw", 1, 2)])
+    fill(T.nb[:, :], 8, -BIG, ["nb"])
+    sel(T.tm8[:, :], T.nb[:, :], [[-16, 8]], A.is_ge, 0, 1, ["nb"], ["tm8"])
+    sel(T.tn8[:, :], T.o8[:, :], [[-16, 8]], A.is_ge, 0, 1, ["o8"], ["tn8"])
+    sel(T.ind[:, :], T.tm8[:, :], [[16, 8]], A.is_ge, 15, -1, ["tm8"], ["ind"])
+    iota(T.LF[96:128, :], [[0, 8], [8192, 64]], C0 - 16 * 8192, 0, [("LF", 1, 2)], True)
+    iota(T.LB[96:128, :], [[0, 8], [-8192, 64]], C0 + 4096 + 16 * 8192, 0, [("LB", 1, 2)], True)
+    iota(T.I97[96:97, :], [[0, 96]], 1, 0, [("I97", 1, 2)], True)
+    sel(T.I97[0:96, :], T.of[0:96, 0:96], [[1, 96]], A.is_equal, 0, -1, ["of"], [("I97", 0, 1)])
+    iota(T.mc[:, :], [[16, 192]], 0, 1, ["mc"])
+    sel(T.Z[:, 15:143:16], T.tn8[:, :], [[16, 8]], A.is_ge, 15, -1, ["tn8"], [("Z", 0, 1)])
+    sel(T.Z[:, 143:176:16], T.tn8[:, 0:3], [[16, 3]], A.is_ge, 15, -1, ["tn8"], [("Z", 1, 2)])
+    for S in ("S1", "S2"):
+        fill(T[S][:, 0:FP], FP, 0, [(S, 0, 3)])
+        fill(T[S][:, FP + W:], FP, 0, [(S, 3 + W, 4000)])
+
+    def lists(t):
+        for u in range(2):
+            vcopy(T.Lit[:, u, 96 * t:96 * t + 96], T.iti[:, 192 * t + u:192 * t + 192:2], ["iti"], [("Lit", 2 * t + u, 2 * t + u + 1)])
+        for u in range(2):
+            vcopy(T.itf[:, u, 1 + 96 * t:97 + 96 * t], T.iti[:, 192 * t + u:192 * t + 192:2], ["iti"], [("itf", 1 + 96 * t + 48 * u, 49 + 96 * t + 48 * u)])
+
+    PIECES = [(1, -1), (0, 0), (1, 0), (0, 1)]
+
+    def keys(t, d, take=True):
+        lst = [(T.X2[0:96, :, :], T.ob[0:1, 0:96], T.crow[0:1, d, :], True, False)]
+        for j in range(d, d + 3):
+            u, s = PIECES[j]
+            a = 1 + 96 * t + s
+            lst.append((T.X2[0:96, :, 16 * j:16 * j + 16], T.itf[:, u, a:a + 96], T.Iw[:, 0:128], False, j == d + 2))
+        mm(lst, ["ob", ("crow", d, d + 1), ("itf", 96 * t, 98 + 96 * t), ("Iw", 0, 1)], ["X2"], [7])
+        if take:
+            keys_out(d)
+
+    def keys_out(d):
+        K = "KB" if d else "KF"
+        acopy(T[K][0:96, :], T.X2[0:96, :, :], ["X2"], [K], [7])
+
+    def rows(t):
+        dmas("y", "rw%d" % t, [(T.Rr[4 * j:128:16, :], T[nm][:, :]) for j, nm in enumerate(("Rhi", "Rge", "Rlo"))], ["Rhi", "Rlo", "Rge"], ["Rr"])
+
+    def window(which):
+        for r in which:
+            acopy(T.Rw[:, r:W:16], T.Rr[:, 192 * r:192 * r + 192], ["Rr"], [("Rw", r, r + 1)])
+
+
+    later = []
+
+    def vote_ops(S, ga, gb, ha, hb, na, nb_, P, side=None):
+        base = (BP if S == "Sb" else FP) - 3
+        H = "Hb" if S == "Sb" else "Hf"
+        Xb = [0, 1] if P == "PA" else [2, 3]
+        n1 = max(na, 1)
+
+        def og():
+            vscan(T[P][:, 0:gb - ga], T.msk[:, 0:gb - ga], T[S][:, base + ga:base + gb], 0.0, A.mult, A.max, ["msk", (S, ga, gb)], [P], Xb)
+
+        def oh():
+            vscan(T[H][:, rev(ha, hb)], T.msk[:, 0:hb - ha], T[S][:, rev(base + ha, base + hb)], 0.0, A.mult, A.max, ["msk", (S, ha, hb)], [(H, ha, hb)])
+
+        def ow():
+            w = T[P][:, n1 + 6 - ga:nb_ + 6 - ga]
+            vtt(w, T[H][:, n1:nb_], w, A.max, [(H, n1, nb_), P], [P], Xb)
+
+        def ov():
+            vtt(T.V[:, n1:nb_], T[S][:, base + 3 + n1:base + 3 + nb_], T[P][:, n1 + 6 - ga:nb_ + 6 - ga], A.is_ge,
+                [(S, n1 + 3, nb_ + 3), P], [("V", n1, nb_)], Xb)
+        if S == "Sb":
+            def og():
+                vscan(T.Gb[:, ga:gb], T.msk[:, 0:gb - ga], T.Sb[:, base + ga:base + gb], 0.0, A.mult, A.max, ["msk", (S, ga, gb)], [("Gb", ga, gb)])
+
+            def carry():
+                mm([(T[P][:, a:b], T.Ib[:, :], T.Gb[:, ga + a:ga + b], True, True) for a, b in ((0, 512), (512, gb - ga))], ["Ib", ("Gb", ga, gb)], [P], Xb)
+            later.append(carry)
+        if side is None:
+            return og, oh, ow, ov
+        Wm, I, J = (side, "Ib", "Jb") if S == "Sb" else (side, "Iw", "Jf")
+
+        def ow2():
+            vtt(T[Wm][:, 0:nb_ - n1], T[H][:, n1:nb_], T[P][:, n1 + 6 - ga:nb_ + 6 - ga], A.max, [(H, n1, nb_), P], [Wm], Xb)
+
+        def ov2():
+            mid = (n1 + nb_) // 2
+            for k, (a, b) in enumerate(((n1, mid), (mid, nb_))):
+                d = T.PB[:, 512 * k:512 * k + b - a]
+                mm([(d, T[I][:, 0:128], T[S][:, base + 3 + a:base + 3 + b], True, False), (d, T[J][:, :], T[Wm][:, a - n1:b - n1], False, True)],
+                   [I, J, (S, a + 3, b + 3), Wm], [("PB", k, k + 1)], [2 + k])
+                op("s", lambda e, a=a, b=b, d=d: e.activation(T.V[:, a:b], d, F.Relu, bias=1.0, scale=2.0 ** 32), [("PB", k, k + 1)], [("V", a, b)], [2 + k])
+        return og, oh, ow2, ov2
+
+    v0 = [vote_ops("Sb", 770 * c, 770 * c + 770, 770 * c, 770 * c + 770, max(770 * c - 6, 0), min(770 * c + 764, W), "PA", ("Wb0", "Wb1", "Wb0", None)[c])
+          for c in range(4)]
+    v0[0][0](); later[0](); v0[0][1]()
+    lists(0)
+    keys(0, 0)
+    v0[1][0](); v0[0][2](); later[1](); v0[0][3]()
+    v0[1][1](); v0[2][0]()
+    vcopy(T.Rhi[:, :], T.roti[:, :], ["roti"], ["Rhi"])
+    v0[1][2](); later[2](); v0[1][3]()
+    vtt(T.Rlo[:, :], T.roti[:, :], T.Rhi[:, :], A.subtract, ["roti", "Rhi"], ["Rlo"])
+    dmas("y", "rw", [(T.Rw[0:128:16, :], T.Rhi[:, :]), (T.Rw[4:128:16, :], T.Rlo[:, :])], ["Rhi", "Rlo"], ["Rw"])
+    vcopy(T.hpf[0:8, 0:3], T.hpi[0:8, 0:3], ["hpi"], ["hpf"])
+    v0[2][1](); v0[3][0]()
+    v0[2][2](); later[3](); v0[2][3]()
+    mm([(T.X0[:, 0:3], T.Ew[0:8, sh:sh + 128], T.hpf[0:8, 0:3], True, True),
+        (T.X0[:, 3:5], T.Ew[0:8, 0:128], T.g8[0:8, :], True, True)], ["Ew", "hpf", "g8"], ["X0"], [5])
+    acopy(T.hv[:, 0:5], T.X0[:, 0:5], ["X0"], ["hv"], [5])
+    keys(0, 1, False)
+    v0[3][1]()
+    v0[3][2](); v0[3][3]()
+
+    for t in range(FR):
+        last = t == FR - 1
+        So = ("Sb", "S1", "S2")[t]
+        Sn = ("S1", "S2", "S1")[t]
+        so = BP if t == 0 else FP
+        Tl = "T0" if t == 0 else "T1"
+        Tt = ("T0", "T1", "T2")[t]
+        Ts, Qu = "Ts%d" % t, "Qu%d" % t
+        turn = 16 * (FR - 1 - t)
+
+        for u in range(2):
+            for h, q in enumerate("vs"):
+                o = T.G[:, 1568 * u + 16 + 768 * h:1568 * u + 16 + 768 * h + 768]
+                w = T.V[:, :].indirect(T.Lit[:, u, 96 * t + 48 * h:96 * t + 48 * h + 48])
+                R, Wr = ["V", ("Lit", 2 * t + u, 2 * t + u + 1)], [("G", 2 * u + h, 2 * u + h + 1)]
+                if q == "v":
+                    vts(o, w, VS, VB, A.mult, A.add, R, Wr)
+                else:
+                    op("s", lambda e, o=o, w=w: e.activation(o, w, F.Identity, bias=VB, scale=VS), R, Wr)
+            lst = []
+            for j, (uu, s) in enumerate(PIECES):
+                if uu == u:
+                    for r in range(16):
+                        a = 1568 * u + 16 * (1 + s) + r
+                        lst.append((T.D[0:96, 16 * j + r:512:64], T.G[:, a:a + 16 * 95 + 1:16], T.ind[:, :], True, True))
+            mm(lst, [("G", 2 * u, 2 * u + 2), ("G", 10, 14), "ind"], ["D"], [4])
+        if t == 0:
+            keys_out(1)
+            zero("Rr", range(2, 3))
+            vts(T.Lm[:, :], T.Lf[:, :], T.hv[:, 3:4], None, A.subtract, None, ["Lf", "hv"], ["Lm"])
+        else:
+            window(range(W1, W2))
+        if not last:
+            lists(t + 1)
+        vscan(T.LF[0:96, 0:496], T.D[0:96, 0:496], T.KF[0:96, 0:496], HUGE, A.min, A.max, ["D", "KF"], [("LF", 0, 1)], [4])
+        vscan(T.LB[0:96, rev(16, 512)], T.D[0:96, rev(16, 512)], T.KB[0:96, rev(16, 512)], HUGE, A.min, A.max, ["D", "KB"], [("LB", 0, 1)], [4])
+        acopy(T.MF[:, :], T.LF[:, 16:496].indirect(T.Lm[:, :]), ["LF", "Lm"], ["MF"])
+        mm([(T.X0[:, u:192:2], T.MF[0:97, 128 * u:128 * u + 128], T.I97[0:97, :], True, True) for u in range(2)], ["MF", "I97"], ["X0"], [5])
+        vcopy(T.MB[:, :], T.LB[:, 16:512].indirect(T.Lm[:, :]), ["LB", "Lm"], ["MB"])
+        mm([(T.X1[:, u:192:2], T.MB[0:97, 128 * u:128 * u + 128], T.I97[0:97, :], True, True) for u in range(2)], ["MB", "I97"], ["X1"], [6])
+        F2, sg, sd, sr = T.PA[:, 0:192], T.PA[:, 192:384], T.PA[:, 512:704], T.PA[:, 704:896]
+        vscan(F2, T.c17[:, :], T.X0[:, 0:192], HUGE, A.add, A.min, ["c17", "X0"], [("PA", 0, 1)], [0, 5])
+        vscan(T.B2[:, ::-1], T.c17[:, :], T.X1[:, 191::-1], HUGE, A.add, A.min, ["c17", "X1"], ["B2"], [6])
+        sg = T.PB[:, 0:192]
+        vtt(T.Dd[:, :], T.B2[:, :], F2, A.subtract, ["B2", ("PA", 0, 1)], ["Dd"], [0])
+        vtt(T.Wi[:, :], T.B2[:, :], F2, A.min, ["B2", ("PA", 0, 1)], ["Wi"], [0])
+        op("s", lambda e, sg=sg: e.activation(sg, T.Dd[:, :], F.Sign), ["Dd"], ["PB"], [2])
+        if t > 0:
+            window(range(W2, 16))
+        else:
+            zero("Rr", range(3, 4))
+        vts(T.di[:, :], T.Wi[:, :], 2.0 ** -13, -C0 / 8192 - 0.4375, A.mult, A.add, ["Wi"], ["di"])
+        vts(T.pi[:, :], T.Wi[:, :], 4095, None, A.bitwise_and, None, ["Wi"], ["pi"])
+        vtt(sd, T.di[:, :], sg, A.mult, ["di", "PB"], [("PA", 2, 3)], [2, 1])
+        vtt(sr, T.pi[:, :], sd, A.add, ["pi", ("PA", 2, 3)], [("PA", 3, 4)], [1])
+        vts(T.Ls[:, :], sr, 0.0, float(W - 1), A.max, A.min, [("PA", 3, 4)], ["Ls"], [1])
+        vtt(T.dm[:, :], T.mc[:, :], sr, A.subtract, ["mc", ("PA", 3, 4)], ["dm"], [1])
+
+        def e_ops():
+            vts(T.ei[:, :], T.dm[:, :], T.hv[:, 3:4], T.hv[:, t:t + 1], A.subtract, A.mult, ["dm", "hv"], ["ei"])
+            vts(T.em[:, :], T.ei[:, :], WC - 1, None, A.bitwise_and, None, ["ei"], ["em"])
+            vcopy(T.ef[:, :], T.em[:, :], ["em"], ["ef"])
+
+        def gb(c):
+            a, b = c
+            acopy(T.Rg[:, 16 * a:16 * b], T.Rw[:, :].indirect(T.Ls[:, a:b]), ["Rw", "Ls"], [("Rg", a, b)])
+
+        def gc(c, q):
+            a, b = c
+            if a >= 144:
+                o, Wr = T[Ts][:, 16 * a - 2304:16 * b - 2304], [(Ts, a, b)]
+            else:
+                o, Wr = T[Tl][:, X + 16 * a:X + 16 * b], [(Tl, X + 16 * a, X + 16 * b)]
+            (vcopy if q == "v" else acopy)(o, T[So][:, so:so + W].indirect(T.Ls[:, a:b]), [So, "Ls"], Wr)
+
+        def ext(c, B):
+            a, b = c
+            o = turn if a >= 144 else 0
+            lst = [(T[B][:, 0:b - a], T.Z[:, 15 - r + o:143 - r + o], T.Rg[:, 16 * a + r:16 * b:16], r == 0, False) for r in range(16)]
+            mm(lst, ["Z", ("Rg", a, b)], [B], [XB[B]])
+            mm([(T[B][:, 0:b - a], T.Iw[:, o:o + 128], T.ef[:, a:b], False, True)], ["Iw", "ef"], [B], [XB[B]])
+
+        def qq(c, B):
+            a, b = c
+            if a >= 144:
+                vcopy(T.Qs[:, 48 * t:48 * t + 48], T[B][:, 0:48], [B], [("Qs", t, t + 1)], [XB[B]])
+                send(T[Qu][:, 0:48], T.Qs[:, 48 * t:48 * t + 48], "aQ%d" % t, [("Qs", t, t + 1)])
+            else:
+                vcopy(T[Qu][:, 48 + a:48 + b], T[B][:, 0:b - a], [B], [(Qu, 48 + a, 48 + b)], [XB[B]])
+
+        def gd(a, b):
+            src, nm = (T[Tt][:, a:b], Tt) if a < X else (T[Tl][:, a:b], Tl)
+            vtt(T[Sn][:, FP + a:FP + b], T.C2[:, :].indirect(T[Qu][:, a // 16:b // 16]), src, A.mult,
+                ["C2", (Qu, a // 16, b // 16), (nm, a, b)], [(Sn, 3 + a, 3 + b)])
+
+        top = (144, 192)
+        arrive("aQ%d" % t, [(Qu, 0, 48)])
+        if not last:
+            c0, c1, c2 = (0, K1), (K1, K2), (K2, 144)
+            n1, n2 = X + 16 * K1, X + 16 * K2
+            j1, j2 = (n1 + 3) // 7 * 7, (n2 + 3) // 7 * 7
+            L, halves = "L%d" % t, t + 1
+            wide = X // halves
+            for i in range(halves):
+                arrive("aT%d%d" % (t, i), [(L, i, i + 1)])
+                dmas("y", "lT%d%d" % (t, i), [(T[Tt][p, wide * i:wide * i + wide], T[L][i, r, :]) for p, r in turned(turn)],
+                     [(L, i, i + 1)], [(Tt, wide * i, wide * i + wide)])
+            P = (("PB", "PA", "PB", "PA"), ("PA", "PA", "PB", "PA"), ("PA", "PA", "PA", "PB"), ("PA", "PA", "PA", "PA"))[PE]
+            side = [("Wf0", "Wf1", "Wf0")[i] if i < PE else None for i in range(3)]
+            va = [vote_ops(Sn, 777, j1, 777, j1, 777, j1 - 6, P[0], side[0]), vote_ops(Sn, j1, j2, j1, j2, j1 - 6, j2 - 6, P[1], side[1]),
+                  vote_ops(Sn, j2, 3080, j2, 3080, j2 - 6, W, P[2], side[2]), vote_ops(Sn, 0, 784, 0, 777, 0, 777, P[3])]
+            gb(c0); e_ops(); gc(c0, CQ); ext(c0, "X0")
+            for i in range(halves):
+                c = (144 + wide * i // 16, 144 + wide * (i + 1) // 16)
+                gc(c, "s")
+                send(T[L][i], T[Ts][:, wide * i:wide * i + wide], "aT%d%d" % (t, i), [(Ts,) + c])
+            qq(c0, "X0"); gd(X, n1)
+            keys(t + 1, 0, False)
+            gb(c1); ext(c1, "X1"); gc(c1, "s"); va[0][0](); va[0][1]()
+            gb(top); ext(top, "X0")
+            qq(c1, "X1"); gd(n1, n2); va[0][2](); qq(top, "X0")
+            gb(c2); ext(c2, "X1"); gc(c2, "s"); keys_out(0)
+            va[1][1]()
+            if PE:
+                va[0][3](); va[1][0]()
+            else:
+                va[1][0](); va[0][3]()
+            qq(c2, "X1"); gd(n2, W)
+            keys(t + 1, 1, False)
+            if RE:
+                va[1][2]()
+            vcopy(T.Qf[:, :], T[Qu][:, :], [Qu], ["Qf"])
+            vts(T.Rge[:, :], T[Qu][:, :], float(WC), -float(WC), A.is_ge, A.mult, [Qu], ["Rge"])
+            acopy(T.Rhi[:, :], T.Qf[:, :], ["Qf"], ["Rhi"])
+            keys_out(1)
+            if RE:
+                va[2][1]()
+            else:
+                va[1][2]()
+            vtt(T.Rlo[:, :], T.Qf[:, :], T.Rhi[:, :], A.subtract, ["Qf", "Rhi"], ["Rlo"])
+            rows(t)
+            if PE >= 2:
+                va[1][3]()
+            if not RE:
+                va[2][1]()
+            va[2][0]()
+            if PE < 2:
+                va[1][3]()
+            va[2][2]()
+            if PE == 3:
+                window(range(W0))
+                va[2][3](); gd(0, X)
+                window(range(W0, W1))
+            else:
+                window(range(W1))
+                gd(0, X); va[2][3]()
+            va[3][0](); va[3][1](); va[3][2](); va[3][3]()
+        else:
+            acc = T.PB
+
+            def fold(parts, start, stop):
+                lst = []
+                for i, (a, b) in enumerate(parts):
+                    lst.append((acc[:, a % 512:a % 512 + b - a], T.Iw[:, 0:128], T[Sn][:, FP + a:FP + b], start and i == 0, stop and i == len(parts) - 1))
+                mm(lst, ["Iw"] + [(Sn, 3 + a, 3 + b) for a, b in parts], ["PB"], [2])
+
+            def store(h):
+                a, b = 256 * h, 256 * h + 256
+                vtt(T.Y[:, a:b], T[Sn][:, FP + a:FP + b], acc[:, a:b], A.add, [(Sn, 3 + a, 3 + b), ("PB", h, h + 1)], [("Y", h, h + 1)], [2])
+                dmas("ys"[h], "y%d" % h, [(T.y[r, a:b], T.Y[p, a:b]) for p, r in lay], [("Y", h, h + 1)], [("out", h, h + 1)])
+
+            c0, c1, c2 = (0, 48), (48, 96), (96, 144)
+            for i, (a, b) in enumerate(((256, X), (0, 256))):
+                gc((144 + a // 16, 144 + b // 16), "s")
+                send(T.T2[:, a:b], T.Ts2[:, a:b], "aT2%d" % i, [(Ts, 144 + a // 16, 144 + b // 16)])
+                arrive("aT2%d" % i, [("T2", a, b)])
+            e_ops(); gb(top); gc(c0, "v"); ext(top, "X0"); gb(c0); gc(c1, "v"); ext(c0, "X1"); qq(top, "X0")
+            gb(c1)
+            if K3 > 96:
+                gc((96, K3), "v")
+            ext(c1, "X0"); qq(c0, "X1"); gd(1024, 2 * X); fold([(1024, 1536)], True, False); gd(X, 1024)
+            gb(c2); ext(c2, "X1")
+            if K3 < 144:
+                gc((K3, 144), "s")
+            fold([(768, 1024)], False, False)
+            if FO == 0:
+                qq(c1, "X0"); gd(2 * X, 2048); fold([(1536, 2048)], False, False); gd(2048, 3 * X); fold([(2048, 2304)], False, False)
+                qq(c2, "X1"); gd(3 * X, 2560); fold([(2304, 2560)], False, True); gd(2560, W)
+            else:
+                qq(c1, "X0"); gd(2 * X, 2048); fold([(1536, 2048)], False, True); qq(c2, "X1"); gd(2048, W)
+                vtt(acc[:, 0:512], T[Sn][:, FP + 2048:FP + 2560], acc[:, 0:512], A.add, [(Sn, 2051, 2563), "PB"], ["PB"], [2])
+            gd(256, X)
+            vtt(acc[:, 0:512], T[Sn][:, FP + 2560:FP + W], acc[:, 0:512], A.add, [(Sn, 2563, 3 + W), "PB"], ["PB"], [2])
+            gd(0, 256)
+            store(1)
+            vtt(acc[:, 0:256], T[Sn][:, FP + 512:FP + X], acc[:, 0:256], A.add, [(Sn, 515, 3 + X), ("PB", 0, 1)], [("PB", 0, 1)], [2])
+            store(0)
+    op("g", lambda e: e.wait_ge(T.sem.sent, sends[0]), ["out"])
+    emit(g, T, ops)

@@ -1,54 +1,63 @@
+import math
+
 from concourse.mybir import AluOpType as A, ActivationFunctionType as F
 
 W, WC, FR, X = 3072, 2048, 3, 768
 HUGE = float(2 ** 26)
 BIG = 2 ** 23
 C0 = -(2 ** 24) + 2 ** 18
-VS, VB = 64.0, -22.0
+MAGIC = 1.5 * 2 ** 23
 FP, BP = 8, 16
 
-K1, K2, CQ, PE, W0, W1, RE, FO = 48, 96, "v", 3, 0, 4, 1, 0
-K3, W2 = 120, 12
+CUT0 = (0, 768, 1536, 2304, W)
+MODE0 = ((2, W), (2, W), (2, 384), (2, 0))
+CUT = (0, 24, 64, 104, 144)
+MODE, SPAN = "ttttttvv", 511
+GC = "vssv" + "v"
+TOP_T, TOP_Q, WG, CHUNK = 0, 1, 8, 512
+CUTL = (0, 48, 96, 144)
+K3, EQ = 96, "vs"
+
+CYCLE, PE_CYCLE, GATHER, HOP, LOCAL, LINK = 0.00083, 0.00043, 1.4, 0.12, 300e3, 70e3
+ROUNDS, ISSUE, FOLD, REMOTE, ROWS, OWN = 2, 0.2, 1, 2.5, 4.0, 0.4
+SLACKS, MV, HEAD = (0.0, 0.1, 0.2, 0.36), 0, 48
+PAIRS, PMODE = 2, ((2, W), (2, W), (2, W), (2, 0), (2, 0))
 
 f32, bf, i32, u16 = "float32", "bfloat16", "int32", "uint16"
 SCRATCH = {
     "Sb": ("sbuf", [128, W + 2 * BP], bf), "S1": ("sbuf", [128, W + 2 * FP], f32), "S2": ("sbuf", [128, W + 2 * FP], f32),
     "T0": ("sbuf", [128, W], bf), "T1": ("sbuf", [128, W], f32), "T2": ("sbuf", [128, X], f32),
     "Ts0": ("sbuf", [128, X], bf), "Ts1": ("sbuf", [128, X], f32), "Ts2": ("sbuf", [128, X], f32),
-    "L0": ("dram", [1, 128, X], bf), "L1": ("dram", [2, 128, X // 2], f32),
     "Qu0": ("sbuf", [128, 192], u16), "Qu1": ("sbuf", [128, 192], u16), "Qu2": ("sbuf", [128, 192], u16),
     "Qs": ("sbuf", [128, 144], u16),
-    "C2": ("sbuf", [128, 2 * WC], bf), "Rw": ("sbuf", [128, W], bf), "Rg": ("sbuf", [128, W], bf),
-    "V": ("sbuf", [128, W], bf), "G": ("sbuf", [128, 2 * 98 * 16], bf),
-    "Hf": ("sbuf", [128, 3080], f32), "Gb": ("sbuf", [128, 3080], bf), "Hb": ("sbuf", [128, 3080], bf), "msk": ("sbuf", [128, 945], bf),
+    "C2": ("sbuf", [128, 2 * WC + 16], bf), "Rw": ("sbuf", [128, W], bf), "Rg": ("sbuf", [128, W], bf),
+    "V": ("sbuf", [128, W], bf), "Cg": ("sbuf", [128, W], bf), "G": ("sbuf", [128, 2 * 98 * 16], bf),
+    "H": ("sbuf", [128, 3080], f32), "M": ("sbuf", [128, 3080], f32),
+    "M2": ("sbuf", [128, 3080], f32), "M4": ("sbuf", [128, 3080], f32), "M7": ("sbuf", [128, 3080], f32),
+    "N2": ("sbuf", [128, 3080], bf), "N4": ("sbuf", [128, 3080], bf), "N7": ("sbuf", [128, 3080], bf),
     "iti": ("sbuf", [128, 576], i32), "Lit": ("sbuf", [128, 2, 288], u16), "itf": ("sbuf", [128, 2, 290], f32),
     "roti": ("sbuf", [128, 192], i32), "hpi": ("sbuf", [128, 4], i32), "hpf": ("sbuf", [128, 4], f32),
-    "g8": ("sbuf", [128, 2], f32), "hv": ("sbuf", [128, 8], f32),
-    "Rhi": ("sbuf", [128, 192], bf), "Rlo": ("sbuf", [128, 192], bf), "Rge": ("sbuf", [128, 192], bf), "Qf": ("sbuf", [128, 192], f32),
+    "g8": ("sbuf", [128, 2], f32), "hv": ("sbuf", [128, 8], f32), "Hd": ("sbuf", [128, 3, 240], f32),
+    "Rhi": ("sbuf", [128, 192], bf), "Rlo": ("sbuf", [128, 192], bf), "Qf": ("sbuf", [128, 192], f32), "Rr": ("sbuf", [128, W], bf),
     "KF": ("sbuf", [128, 512], f32), "KB": ("sbuf", [128, 512], f32),
-    "LF": ("sbuf", [128, 512], f32), "LB": ("sbuf", [128, 512], f32),
-    "MF": ("sbuf", [128, 256], f32), "MB": ("sbuf", [128, 256], f32),
-    "Lf": ("sbuf", [128, 16], f32), "Lm": ("sbuf", [128, 16], u16),
+    "LF": ("sbuf", [128, 512], f32), "LB": ("sbuf", [128, 512], f32), "Lf": ("sbuf", [128, 16], f32), "Lm": ("sbuf", [128, 16], u16),
+    "MF": ("sbuf", [128, 2, 128], f32), "MB": ("sbuf", [128, 2, 128], f32),
     "B2": ("sbuf", [128, 192], f32), "Wi": ("sbuf", [128, 192], i32), "Dd": ("sbuf", [128, 192], f32),
     "pi": ("sbuf", [128, 192], i32), "di": ("sbuf", [128, 192], i32), "Ls": ("sbuf", [128, 192], u16),
-    "dm": ("sbuf", [128, 192], f32), "ei": ("sbuf", [128, 192], i32), "em": ("sbuf", [128, 192], i32), "ef": ("sbuf", [128, 192], f32),
-    "c17": ("sbuf", [128, 192], f32), "mc": ("sbuf", [128, 192], f32),
-    "of": ("sbuf", [128, 256], f32), "ob": ("sbuf", [128, 96], bf), "o8": ("sbuf", [128, 8], bf), "nb": ("sbuf", [128, 8], bf),
-    "Iw": ("sbuf", [128, 160], f32), "I97": ("sbuf", [128, 96], f32), "Ew": ("sbuf", [128, 256], f32),
-    "ind": ("sbuf", [128, 8], bf), "tm8": ("sbuf", [128, 8], bf), "tn8": ("sbuf", [128, 8], bf),
-    "Z": ("sbuf", [128, 176], bf), "Rr": ("sbuf", [128, W], bf), "crow": ("sbuf", [128, 2, 512], bf),
-    "Wb0": ("sbuf", [128, 784], bf), "Wb1": ("sbuf", [128, 784], bf), "Wf0": ("sbuf", [128, 944], f32), "Wf1": ("sbuf", [128, 944], f32),
-    "Ib": ("sbuf", [128, 128], bf), "Jb": ("sbuf", [128, 128], bf), "Jf": ("sbuf", [128, 128], f32),
+    "b2": ("sbuf", [128, 192], f32), "Rk": ("sbuf", [128, 192], bf), "dm": ("sbuf", [128, 192], f32), "a2": ("sbuf", [128, 192], f32), "Kw": ("sbuf", [128, 240], f32), "krow": ("sbuf", [128, 64], bf),
+    "c17": ("sbuf", [128, 192], f32), "mc": ("sbuf", [128, 192], f32), "mp": ("sbuf", [128, 192], f32),
+    "of": ("sbuf", [128, 128], f32), "ob": ("sbuf", [128, 128], bf), "nb": ("sbuf", [128, 8], bf),
+    "Iw": ("sbuf", [128, 240], f32), "I97": ("sbuf", [128, 96], f32), "Ew": ("sbuf", [128, 128], f32),
+    "ind": ("sbuf", [128, 8], bf), "tm8": ("sbuf", [128, 8], bf),
+    "Z": ("sbuf", [128, 256], bf), "crow": ("sbuf", [128, 2, 512], bf), "brow": ("sbuf", [128, 512], bf),
+    "Jb": ("sbuf", [128, 128], bf), "Db": ("sbuf", [128, 128], bf),
+    "Jf": ("sbuf", [128, 128], f32), "Df": ("sbuf", [128, 128], f32),
     "Y": ("sbuf", [128, 512], f32),
     "PA": ("psum", [128, 1024], f32), "PB": ("psum", [128, 1024], f32), "D": ("psum", [128, 512], f32),
     "X0": ("psum", [128, 512], f32), "X1": ("psum", [128, 512], f32), "X2": ("psum", [128, 8, 64], f32),
 }
 SEMAPHORES = ["qv", "qs", "qt", "qg", "sent", "sp0", "sp1", "sp2", "sp3", "rec", "itg", "rot", "hop", "rw", "rw0", "rw1",
-              "aT00", "aT10", "aT11", "aT20", "aT21", "aQ0", "aQ1", "aQ2", "lT00", "lT10", "lT11", "y0", "y1"]
-
-
-def rev(lo, hi):
-    return slice(hi - 1, lo - 1 if lo > 0 else None, -1)
+              "aT00", "aT10", "aT11", "aT20", "aT21", "aQ0", "aQ1", "aQ2", "y0", "y1"]
 
 
 def meets(a, b):
@@ -57,6 +66,99 @@ def meets(a, b):
 
 def tok(x):
     return (x, 0, 1 << 30) if isinstance(x, str) else x
+
+
+def count(ap):
+    return math.prod(ap.shape[1:])
+
+
+def width(name):
+    return 2 if name in SCRATCH and SCRATCH[name][2] in (bf, u16) else 4
+
+
+def size(ap):
+    return ap.shape[0] * count(ap) * (width(ap.name) if ap.name in SCRATCH else 4)
+
+
+def clash(p, o):
+    return (any(meets(a, b) for a in p["W"] for b in o["R"] + o["W"]) or any(meets(a, b) for a in p["R"] for b in o["W"])
+            or (p["q"] != o["q"] and any(b in p["X"] for b in o["X"])))
+
+
+def arrange(ops):
+    n = len(ops)
+    seen, before = {}, []
+    for i, o in enumerate(ops):
+        names = {a[0] for a in o["R"] + o["W"]} | set(o["X"])
+        before.append(sorted(j for j in set().union(*[seen.get(x, ()) for x in names]) if clash(ops[j], o)))
+        o["needs"] = [ops[j] for j in before[i]]
+        for x in names:
+            seen.setdefault(x, []).append(i)
+    for i, o in enumerate(ops):
+        if o["tag"]:
+            k = [j for j, p in enumerate(ops) if p["q"] is None and p["sem"] == o["tag"][0]][0]
+            before[k].append(i)
+            before[n - 1].append(i)
+            ops[k]["busy"] = o["tag"][1]
+    after = [[] for o in ops]
+    for i in range(n):
+        for j in before[i]:
+            after[j].append(i)
+    def gap(j, i):
+        return ops[j]["late"] + (HOP if ops[j]["q"] != ops[i]["q"] else 0.0 if ops[i]["q"] == "t" else OWN)
+
+    def place(key, back):
+        pre, post = (after, before) if back else (before, after)
+        left = [len(b) for b in pre]
+        ready = {i for i in range(n) if not left[i]}
+        taken, end = {}, [0.0] * n
+        while ready:
+            i = min(ready, key=lambda k: (key[k], k))
+            ready.remove(i)
+            at = max([end[j] + (gap(i, j) if back else gap(j, i)) for j in pre[i]], default=0.0)
+            line = taken.setdefault(ops[i]["q"], [])
+            k = 0
+            while k < len(line) and line[k][0] < at + ops[i]["busy"] - 1e-9:
+                at = max(at, line[k][1])
+                k += 1
+            line.insert(k, (at, at + ops[i]["busy"]))
+            end[i] = at + ops[i]["busy"]
+            for k in post[i]:
+                left[k] -= 1
+                if not left[k]:
+                    ready.add(k)
+        return end
+
+    def run(key, slack, back):
+        pre, post = (after, before) if back else (before, after)
+        left = [len(b) for b in pre]
+        ready = {i: 0.0 for i in range(n) if not left[i]}
+        free, end = {}, [0.0] * n
+        while ready:
+            start = {i: max(r, free.get(ops[i]["q"], 0.0)) for i, r in ready.items()}
+            first = min(start, key=lambda i: (start[i], key[i]))
+            q = ops[first]["q"]
+            i = min((key[k], k) for k in start if ops[k]["q"] == q and start[k] <= start[first] + slack)[1]
+            end[i] = free[q] = start[i] + ops[i]["busy"]
+            del ready[i]
+            for k in post[i]:
+                left[k] -= 1
+                if not left[k]:
+                    ready[k] = max(end[j] + (gap(k, j) if back else gap(j, k)) for j in pre[k])
+        return end
+
+    end = place(list(range(n)), False)
+    best = end
+    for turn in range(ROUNDS):
+        late = [-x for x in place([-x for x in end], True)]
+        end = min([place(late, False)] + [run(late, s, False) for s in SLACKS], key=max)
+        if max(end) < max(best):
+            best = end
+        late = [-x for x in min([run([-x for x in end], s, True) for s in SLACKS], key=max)]
+        end = min([place(late, False)] + [run(late, s, False) for s in SLACKS], key=max)
+        if max(end) < max(best):
+            best = end
+    return [ops[i] for i in sorted(range(n), key=lambda i: (-1, i) if ops[i]["q"] and ops[i]["sem"] and not before[i] else (best[i] - ops[i]["busy"], best[i]))]
 
 
 def emit(g, T, ops):
@@ -71,21 +173,16 @@ def emit(g, T, ops):
             pos[q] += 1
         else:
             o["src"], o["pos"] = "d" + o["sem"], 0
-        o["waits"] = []
+        o["waits"], o["at"] = [], i
         if q is None:
             o["known"] = {}
             continue
         deps = {}
-        for j in range(i):
-            p = ops[j]
-            same = p["q"] == q and p["sem"] is None and o["sem"] is None
-            if same and q == "t":
+        for p in o["needs"]:
+            if p["q"] == q == "t":
                 continue
-            hit = any(meets(a, b) for a in p["W"] for b in o["R"] + o["W"]) or any(meets(a, b) for a in p["R"] for b in o["W"])
-            if not hit and p["q"] != q:
-                hit = any(b in p["X"] for b in o["X"])
-            if hit and (p["src"] not in deps or ops[deps[p["src"]]]["pos"] < p["pos"]):
-                deps[p["src"]] = j
+            if p["src"] not in deps or ops[deps[p["src"]]]["pos"] < p["pos"]:
+                deps[p["src"]] = p["at"]
         for j in sorted(deps.values(), reverse=True):
             p = ops[j]
             if known[q].get(p["src"], -1) >= p["pos"]:
@@ -126,221 +223,250 @@ def rank_program(g, core, T, topo):
     rid, pid = topo.addr(nxt, core)
     out_mask, n_out, n_in = topo.mask(core, nxt), len(topo.engines(core, nxt)), len(topo.engines(prv, core))
     ops = []
-    sends = [0]
+    sends, loaded = [0], [0.0]
 
-    def op(q, fn, R=(), Wr=(), Xb=(), sem=None, n=0):
-        ops.append({"q": q, "fn": fn, "R": [tok(x) for x in R], "W": [tok(x) for x in Wr], "X": list(Xb), "sem": sem, "n": n})
-
-    def turned(shift):
-        if shift == 0:
-            return [(slice(0, 128), slice(0, 128))]
-        return [(slice(0, 128 - shift), slice(shift, 128)), (slice(128 - shift, 128), slice(0, shift))]
+    def op(q, fn, R=(), Wr=(), Xb=(), sem=None, n=0, busy=0.0, late=0.0, tag=None, rank=0):
+        ops.append({"q": q, "fn": fn, "R": [tok(x) for x in R], "W": [tok(x) for x in Wr], "X": list(Xb), "sem": sem, "n": n,
+                    "busy": busy, "late": late, "tag": tag, "rank": rank})
 
     def dmas(q, sem, pairs, R, Wr):
-        op(q, lambda e: [e.dma_start(a, b) for a, b in pairs], R, Wr, sem=sem, n=16 * len(pairs))
+        op(q, lambda e: [e.dma_start(a, b) for a, b in pairs], R, Wr, sem=sem, n=16 * len(pairs),
+           busy=ISSUE * len(pairs), late=1.6 + loaded[0] + sum(size(a) for a, b in pairs) / LOCAL)
+        if not R:
+            loaded[0] = ops[-1]["late"] - 1.6
 
     def send(dst, src, sem, R):
         sends[0] += n_out
-        op("g", lambda e: e.remote_dma(dst, src, T.sem[sem], T.sem.sent, pid, rid, out_mask), R)
+        op("g", lambda e: e.remote_dma(dst, src, T.sem[sem], T.sem.sent, pid, rid, out_mask), R,
+           busy=0.3, late=REMOTE, tag=(sem, size(src) / LINK))
 
     def arrive(sem, Wr):
         op(None, None, (), Wr, sem=sem, n=n_in)
 
-    def vmem(ap, val, Wr):
-        op("v", lambda e: e.memset(ap, val), (), Wr)
+    def vec(fn, o, R, Wr, Xb, rate=None):
+        if rate is None:
+            rate = 0.5 if all(width(tok(x)[0]) == 2 for x in list(R) + list(Wr)) else 1.0
+        op("v", fn, R, Wr, Xb, busy=0.05 + count(o) * rate * CYCLE)
 
-    def vcopy(o, i, R, Wr, Xb=()):
-        op("v", lambda e: e.tensor_copy(o, i), R, Wr, Xb)
+    def vmem(ap, val, Wr, Xb=()):
+        vec(lambda e: e.memset(ap, val), ap, (), Wr, Xb, 0.5 if width(ap.name) == 2 else 1.0)
 
-    def vtt(o, a, b, alu, R, Wr, Xb=()):
-        op("v", lambda e: e.tensor_tensor(o, a, b, alu), R, Wr, Xb)
+    def vcopy(o, i, R, Wr, Xb=(), rate=None):
+        vec(lambda e: e.tensor_copy(o, i), o, R, Wr, Xb, rate)
 
-    def vts(o, a, s1, s2, o0, o1, R, Wr, Xb=()):
+    def vtt(o, a, b, alu, R, Wr, Xb=(), rate=None):
+        vec(lambda e: e.tensor_tensor(o, a, b, alu), o, R, Wr, Xb, rate or (1.0 if Xb else 2.0))
+
+    def vts(o, a, s1, s2, o0, o1, R, Wr, Xb=(), rate=None):
         if s2 is None:
-            op("v", lambda e: e.tensor_scalar(o, a, s1, None, o0), R, Wr, Xb)
+            vec(lambda e: e.tensor_scalar(o, a, s1, None, o0), o, R, Wr, Xb, rate)
         else:
-            op("v", lambda e: e.tensor_scalar(o, a, s1, s2, o0, o1), R, Wr, Xb)
+            vec(lambda e: e.tensor_scalar(o, a, s1, s2, o0, o1), o, R, Wr, Xb, rate)
 
     def vscan(o, a, b, init, o0, o1, R, Wr, Xb=()):
-        op("v", lambda e: e.tensor_tensor_scan(o, a, b, init, o0, o1), R, Wr, Xb)
+        vec(lambda e: e.tensor_tensor_scan(o, a, b, init, o0, o1), o, R, Wr, Xb)
 
-    def acopy(o, i, R, Wr, Xb=()):
-        op("s", lambda e: e.activation(o, i, F.Copy), R, Wr, Xb)
+    def act(o, i, R, Wr, Xb=(), fn=F.Copy, rate=1.0, first=False, later=False, **k):
+        op("s", lambda e: e.activation(o, i, fn, **k), R, Wr, Xb, busy=0.065 + count(o) * rate * CYCLE, rank=later - first)
 
-    def mm(lst, R, Wr, Xb):
+    def affine(q, o, i, scale, bias, R, Wr):
+        if q == "v":
+            vts(o, i, scale, bias, A.mult, A.add, R, Wr)
+        else:
+            act(o, i, R, Wr, fn=F.Identity, scale=scale, bias=bias)
+
+    def mm(lst, R, Wr, Xb, first=False):
         def fn(e):
             r = None
             for a in lst:
                 r = e.matmul(*a)
             return r
-        op("t", fn, R, Wr, Xb)
+        cycles = sum(max(min(64, count(a[1])), count(a[2])) * (4 if width(a[1].name) == 4 else 1) for a in lst)
+        op("t", fn, R, Wr, Xb, busy=cycles * PE_CYCLE, rank=-first)
 
-    def iota(o, pat, base, cm, Wr, high=False):
-        op("g", lambda e: e.iota(o, pat, base, cm, allow_small_or_imprecise_dtypes=True), [] if high else ["pool"], Wr + (["pool"] if high else []))
+    def iota(o, pat, base, cm, Wr):
+        op("g", lambda e: e.iota(o, pat, base, cm, allow_small_or_imprecise_dtypes=True), (), Wr, busy=0.13 + 2 * count(o) * CYCLE)
 
     def sel(o, i, pat, cmp, base, cm, R, Wr):
-        op("g", lambda e: e.affine_select(o, i, pat, cmp, 0.0, base, cm), R + ["pool"], Wr)
+        op("g", lambda e: e.affine_select(o, i, pat, cmp, 0.0, base, cm), R, Wr, busy=0.17 + 2 * count(o) * CYCLE)
 
-    XB = {"X0": 5, "X1": 6, "X2": 7}
-    sh = (32 * rank) % 128
-    lay = turned(sh)
+    XB = {"X0": 5, "X1": 6, "X2": 7, "D": 4}
 
-    cuts = [0, 768, 1544, 2312, W]
     for c in range(4):
-        a, b = cuts[c], cuts[c + 1]
-        dmas("y", "sp%d" % c, [(T.Sb[p, BP + a:BP + b], T.sp[r, a:b]) for p, r in lay], (), [("Sb", 3 + a, 3 + b)])
-    dmas("s", "hop", [(T.hpi[0:8, 0:3], T.hop[:, :])], (), ["hpi"])
-    dmas("s", "rot", [(T.roti[p, :], T.rot[r.start // 16:r.stop // 16, :]) for p, r in lay], (), ["roti"])
-    dmas("s", "itg", [(T.iti[p, :], T.itg[r, :]) for p, r in lay], (), ["iti"])
-    dmas("y", "rec", [(T.C2[p, k * WC:(k + 1) * WC], T.rec[r, :]) for k in range(2) for p, r in lay], (), ["C2"])
+        a, b = CUT0[c], CUT0[c + 1]
+        dmas("ys"[c % 2], "sp%d" % c, [(T.Sb[:, BP + a:BP + b], T.sp[:, a:b])], (), [("Sb", 3 + a, 3 + b)])
+    dmas("y", "itg", [(T.iti[:, :], T.itg[:, :])], (), ["iti"])
+    dmas("s", "rot", [(T.roti[:, :], T.rot[:, :])], (), ["roti"])
+    dmas("y", "hop", [(T.hpi[0:8, 0:3], T.hop[:, :])], (), ["hpi"])
+    dmas("y", "rec", [(T.C2[:, k * WC:(k + 1) * WC], T.rec[:, :]) for k in range(2)], (), [("C2", 0, 2 * WC)])
+
+    loaded[0] = 0.0
 
     vmem(T.of[:, :], 1.0, ["of"])
-    vmem(T.msk[:, :], 1.0, ["msk"])
     vmem(T.Sb[:, 0:BP], 0.0, [("Sb", 0, 3)])
     vmem(T.Sb[:, BP + W:], 0.0, [("Sb", 3 + W, 4000)])
-    vmem(T.msk[:, 0:945:7], 0.0, ["msk"])
-    vmem(T.o8[:, :], 1.0, ["o8"])
+    vmem(T.nb[:, :], -float(BIG), ["nb"])
+    vmem(T.ob[0:1, :], 8192.0, ["ob"])
+    vmem(T.krow[0:1, :], 2048.0 * MAGIC / 8192, ["krow"])
+    vmem(T.brow[0:1, :], 352.0 * BIG / 8192, ["brow"])
+    vmem(T.itf[:, :, 0:290:289], 0.0, [("itf", a, a + 1) for a in (0, 289, 290, 579)])
+    vmem(T.itf[:, :, 97:194:96], 0.0, [("itf", a, a + 1) for a in (97, 193, 387, 483)])
+    vmem(T.I97[96:97, :], 1.0, [("I97", 1, 2)])
+    vmem(T.Rw[:, :], 0.0, ["Rw"])
     vmem(T.Z[:, :], 0.0, ["Z"])
-    vmem(T.V[:, 0:1], 1.0, [("V", 0, 1)])
+    vmem(T.V[:, 0:1], 0.0, [("V", 0, 1)])
     for u in range(2):
-        vmem(T.G[:, 1568 * u:1568 * u + 16], -1.0, [("G", 10 + 2 * u, 11 + 2 * u)])
-        vmem(T.G[:, 1568 * u + 1552:1568 * u + 1568], -1.0, [("G", 11 + 2 * u, 12 + 2 * u)])
+        vmem(T.G[:, 1568 * u:1568 * u + 16], 0.0, [("G", 10 + 2 * u, 11 + 2 * u)])
+        vmem(T.G[:, 1568 * u + 1552:1568 * u + 1568], 0.0, [("G", 11 + 2 * u, 12 + 2 * u)])
     vmem(T.c17[:, :], float(2 ** 17), ["c17"])
 
-    def fill(o, n, val, Wr):
-        iota(o, [[0, n]], val, 0, Wr)
-
-    def zero(nm, which):
-        for c in which:
-            op("s", lambda e, a=X * c: e.activation(T[nm][:, a:a + X], T.msk[:, 0:X], F.Copy, scale=0.0), ["msk"], [(nm, 4 * c, 4 * c + 4)])
-
     sel(T.Iw[:, 0:128], T.of[:, 0:128], [[1, 128]], A.is_equal, 0, -1, ["of"], [("Iw", 0, 1)])
-    acopy(T.Ib[:, :], T.Iw[:, 0:128], [("Iw", 0, 1)], ["Ib"])
-    op("s", lambda e: e.activation(T.Jb[:, :], T.Iw[:, 0:128], F.Copy, scale=-1.0), [("Iw", 0, 1)], ["Jb"])
-    op("s", lambda e: e.activation(T.Jf[:, :], T.Iw[:, 0:128], F.Copy, scale=-1.0), [("Iw", 0, 1)], ["Jf"])
-    zero("Rw", range(4))
-    zero("Rr", range(2))
-    iota(T.crow[0:1, 0, :], [[0, 8], [-1, 64]], 16, 0, [("crow", 0, 1)])
-    fill(T.ob[0:1, :], 96, 8192, ["ob"])
-    iota(T.itf[:, :, 0:290:289], [[0, 2], [0, 2]], 0, 0, [("itf", 0, 1), ("itf", 289, 290)])
-    iota(T.itf[:, :, 97:194:96], [[0, 2], [0, 2]], 0, 0, [("itf", 97, 98), ("itf", 193, 194)])
-    fill(T.crow[0:1, 0, 0:512:64], 8, int(HUGE) // 8192, [("crow", 0, 1)])
-    iota(T.crow[0:1, 1, :], [[0, 8], [1, 64]], -16, 0, [("crow", 1, 2)])
-    fill(T.crow[0:1, 1, 63:512:64], 8, int(HUGE) // 8192, [("crow", 1, 2)])
-    sel(T.Ew[0:8, :], T.of[0:8, :], [[0, 2], [1, 128]], A.is_ge, 0, -16, ["of"], ["Ew"])
-    iota(T.g8[0:8, :], [[0, 2]], 0, 16, ["g8"])
-    sel(T.Ew[0:8, :], T.Ew[0:8, :], [[0, 2], [-1, 128]], A.is_ge, 15, 16, ["Ew"], ["Ew"])
-    iota(T.Lf[:, :], [[16, 2], [64, 8]], 0, 1, ["Lf"])
-    sel(T.Iw[:, 128:160], T.of[:, 0:32], [[1, 32]], A.is_equal, 0, -1, ["of"], [("Iw", 1, 2)])
-    fill(T.nb[:, :], 8, -BIG, ["nb"])
+    for nm, k in (("Db", 2.0), ("Jb", -1.0)):
+        act(T[nm][:, :], T.Iw[:, 0:128], [("Iw", 0, 1)], [nm], scale=k)
+    iota(T.crow[:, 0, :], [[0, 8], [-1, 64]], 16, 0, [("crow", 0, 1)])
+    act(T.crow[0:1, 1, :], T.crow[0:1, 0, :], [("crow", 0, 1)], [("crow", 1, 2)], scale=-1.0)
+    affine("s", T.LF[96:128, :], T.crow[96:128, 0, :], -8192.0, float(C0), [("crow", 0, 1)], [("LF", 1, 2)])
+    affine("s", T.LB[96:128, :], T.crow[96:128, 0, :], 8192.0, float(C0 + 4096), [("crow", 0, 1)], [("LB", 1, 2)])
+    vmem(T.crow[0:1, 0, 0:512:64], HUGE / 8192, [("crow", 0, 1)])
+    vmem(T.crow[0:1, 1, 63:512:64], HUGE / 8192, [("crow", 1, 2)])
     sel(T.tm8[:, :], T.nb[:, :], [[-16, 8]], A.is_ge, 0, 1, ["nb"], ["tm8"])
-    sel(T.tn8[:, :], T.o8[:, :], [[-16, 8]], A.is_ge, 0, 1, ["o8"], ["tn8"])
     sel(T.ind[:, :], T.tm8[:, :], [[16, 8]], A.is_ge, 15, -1, ["tm8"], ["ind"])
-    iota(T.LF[96:128, :], [[0, 8], [8192, 64]], C0 - 16 * 8192, 0, [("LF", 1, 2)], True)
-    iota(T.LB[96:128, :], [[0, 8], [-8192, 64]], C0 + 4096 + 16 * 8192, 0, [("LB", 1, 2)], True)
-    iota(T.I97[96:97, :], [[0, 96]], 1, 0, [("I97", 1, 2)], True)
-    sel(T.I97[0:96, :], T.of[0:96, 0:96], [[1, 96]], A.is_equal, 0, -1, ["of"], [("I97", 0, 1)])
-    iota(T.mc[:, :], [[16, 192]], 0, 1, ["mc"])
-    sel(T.Z[:, 15:143:16], T.tn8[:, :], [[16, 8]], A.is_ge, 15, -1, ["tn8"], [("Z", 0, 1)])
-    sel(T.Z[:, 143:176:16], T.tn8[:, 0:3], [[16, 3]], A.is_ge, 15, -1, ["tn8"], [("Z", 1, 2)])
+    sel(T.Ew[0:8, :], T.of[0:8, :], [[1, 128]], A.is_ge, 0, -16, ["of"], ["Ew"])
+    iota(T.g8[0:8, :], [[0, 2]], 0, -16, ["g8"])
+    sel(T.Ew[0:8, :], T.Ew[0:8, :], [[-1, 128]], A.is_ge, 15, 16, ["Ew"], ["Ew"])
+    iota(T.Lf[:, :], [[16, 2], [64, 8]], 0, 1, ["Lf"])
+    iota(T.mp[:, :], [[16, 192]], 0, 1, ["mp"])
+    act(T.I97[0:96, :], T.Iw[0:96, 0:96], [("Iw", 0, 1)], [("I97", 0, 1)])
+    act(T.Iw[:, 128:240], T.Iw[:, 0:112], [("Iw", 0, 1)], [("Iw", 1, 2)])
+    for k in range(2):
+        act(T.Z[:, 15 + 128 * k:128 + 128 * k:16], T.ind[:, :], ["ind"], [("Z", k, k + 1)], scale=-1.0 / BIG)
     for S in ("S1", "S2"):
-        fill(T[S][:, 0:FP], FP, 0, [(S, 0, 3)])
-        fill(T[S][:, FP + W:], FP, 0, [(S, 3 + W, 4000)])
+        vmem(T[S][:, 0:FP], 0.0, [(S, 0, 3)])
+        vmem(T[S][:, FP + W:], 0.0, [(S, 3 + W, 4000)])
 
-    def lists(t):
+    def offsets(t):
         for u in range(2):
             vcopy(T.Lit[:, u, 96 * t:96 * t + 96], T.iti[:, 192 * t + u:192 * t + 192:2], ["iti"], [("Lit", 2 * t + u, 2 * t + u + 1)])
+
+    def targets(t):
         for u in range(2):
-            vcopy(T.itf[:, u, 1 + 96 * t:97 + 96 * t], T.iti[:, 192 * t + u:192 * t + 192:2], ["iti"], [("itf", 1 + 96 * t + 48 * u, 49 + 96 * t + 48 * u)])
+            vcopy(T.itf[:, u, 1 + 96 * t:97 + 96 * t], T.iti[:, 192 * t + u:192 * t + 192:2], ["iti"], [("itf", 290 * u + 1 + 96 * t, 290 * u + 97 + 96 * t)])
 
     PIECES = [(1, -1), (0, 0), (1, 0), (0, 1)]
 
-    def keys(t, d, take=True):
-        lst = [(T.X2[0:96, :, :], T.ob[0:1, 0:96], T.crow[0:1, d, :], True, False)]
+    def keys(t, d, B):
+        lst = [(T[B][0:96, :, :], T.ob[0:1, 0:96], T.crow[0:1, d, :], True, False)]
         for j in range(d, d + 3):
             u, s = PIECES[j]
             a = 1 + 96 * t + s
-            lst.append((T.X2[0:96, :, 16 * j:16 * j + 16], T.itf[:, u, a:a + 96], T.Iw[:, 0:128], False, j == d + 2))
-        mm(lst, ["ob", ("crow", d, d + 1), ("itf", 96 * t, 98 + 96 * t), ("Iw", 0, 1)], ["X2"], [7])
-        if take:
-            keys_out(d)
+            lst.append((T[B][0:96, :, 16 * j:16 * j + 16], T.itf[:, u, a:a + 96], T.Iw[:, 0:128], False, j == d + 2))
+        mm(lst, ["ob", ("crow", d, d + 1), ("itf", 96 * t, 98 + 96 * t), ("itf", 290 + 96 * t, 388 + 96 * t), ("Iw", 0, 1)], [B], [XB[B]])
 
-    def keys_out(d):
+    def keys_out(d, B):
         K = "KB" if d else "KF"
-        acopy(T[K][0:96, :], T.X2[0:96, :, :], ["X2"], [K], [7])
+        act(T[K][0:96, :], T[B][0:96, :, :], [B], [K], [XB[B]])
 
-    def rows(t):
-        dmas("y", "rw%d" % t, [(T.Rr[4 * j:128:16, :], T[nm][:, :]) for j, nm in enumerate(("Rhi", "Rge", "Rlo"))], ["Rhi", "Rlo", "Rge"], ["Rr"])
+    def rows(t, to, B):
+        act(T.Rhi[:, :], T.Qf[:, :], ["Qf"], ["Rhi"])
+        mm([(T[B][:, 0:192], T.Iw[:, 0:128], T.Qf[:, :], True, False), (T[B][:, 0:192], T.Jb[:, :], T.Rhi[:, :], False, True)],
+           ["Rhi", "Qf", "Jb", ("Iw", 0, 1)], [B], [XB[B]])
+        act(T.Rlo[:, :], T[B][:, 0:192], [B], ["Rlo"], [XB[B]])
+        affine("s", T.b2[:, :], T.Qf[:, :], 2.0 ** -11, MAGIC, ["Qf"], ["b2"])
+        affine("s", T.Rk[:, :], T.b2[:, :], -2048.0, 2048.0 * MAGIC, ["b2"], ["Rk"])
+        dmas("y", "rw%s" % t, [(T[to][4 * j:128:16, :], T[nm][:, :]) for j, nm in enumerate(("Rhi", "Rk", "Rlo"))], ["Rhi", "Rlo", "Rk"], [to])
+        ops[-1]["late"] = ROWS
 
     def window(which):
         for r in which:
-            acopy(T.Rw[:, r:W:16], T.Rr[:, 192 * r:192 * r + 192], ["Rr"], [("Rw", r, r + 1)])
+            if r < WG:
+                sel(T.Rw[:, r:W:16], T.Rr[:, 192 * r:192 * r + 192], [[0, 192]], A.is_ge, 0, 0, ["Rr"], [("Rw", r, r + 1)])
+            else:
+                act(T.Rw[:, r:W:16], T.Rr[:, 192 * r:192 * r + 192], ["Rr", ("G", 3, 4)], [("Rw", r, r + 1)], later=True)
 
+    banks = [0]
 
-    later = []
+    def votes(S, ja, jb, mode, closed=False):
+        b16 = S == "Sb"
+        base = (BP if b16 else FP) - 3
+        M2, M4, M7 = ("N2", "N4", "N7") if b16 else ("M2", "M4", "M7")
+        I, J, D2 = ("Ib", "Jb", "Db") if b16 else ("Iw", "Jf", "Df")
+        first = ja in (0, X + 3) if not b16 else ja == 0
+        a2, a4, an = (ja, ja, max(ja, 1)) if first else (ja - 1, ja - 3, ja - 6)
+        b2, b4, bn = (jb, jb, jb) if closed else (jb - 1, jb - 3, jb - 6)
 
-    def vote_ops(S, ga, gb, ha, hb, na, nb_, P, side=None):
-        base = (BP if S == "Sb" else FP) - 3
-        H = "Hb" if S == "Sb" else "Hf"
-        Xb = [0, 1] if P == "PA" else [2, 3]
-        n1 = max(na, 1)
+        def m2():
+            vscan(T[M2][:, a2:b2], T[S][:, base + a2:base + b2], T[S][:, base + a2 + 1:base + b2 + 1], HUGE, A.min, A.max, [(S, a2, b2 + 1)], [(M2, a2, b2)])
 
-        def og():
-            vscan(T[P][:, 0:gb - ga], T.msk[:, 0:gb - ga], T[S][:, base + ga:base + gb], 0.0, A.mult, A.max, ["msk", (S, ga, gb)], [P], Xb)
+        def m4():
+            vscan(T[M4][:, a4:b4], T[M2][:, a4:b4], T[M2][:, a4 + 2:b4 + 2], HUGE, A.min, A.max, [(M2, a4, b4 + 2)], [(M4, a4, b4)])
 
-        def oh():
-            vscan(T[H][:, rev(ha, hb)], T.msk[:, 0:hb - ha], T[S][:, rev(base + ha, base + hb)], 0.0, A.mult, A.max, ["msk", (S, ha, hb)], [(H, ha, hb)])
+        def m7(a, b):
+            vscan(T[M7][:, a:b], T[M4][:, a:b], T[M4][:, a + 3:b + 3], HUGE, A.min, A.max, [(M4, a, b + 3)], [(M7, a, b)])
 
-        def ow():
-            w = T[P][:, n1 + 6 - ga:nb_ + 6 - ga]
-            vtt(w, T[H][:, n1:nb_], w, A.max, [(H, n1, nb_), P], [P], Xb)
+        def diff(a, b):
+            vscan(T.V[:, a:b], T[S][:, base + 3 + a:base + 3 + b], T[M7][:, a:b], 0.0, A.max, A.subtract, [(S, a + 3, b + 3), (M7, a, b)], [("V", a, b)])
 
-        def ov():
-            vtt(T.V[:, n1:nb_], T[S][:, base + 3 + n1:base + 3 + nb_], T[P][:, n1 + 6 - ga:nb_ + 6 - ga], A.is_ge,
-                [(S, n1 + 3, nb_ + 3), P], [("V", n1, nb_)], Xb)
-        if S == "Sb":
-            def og():
-                vscan(T.Gb[:, ga:gb], T.msk[:, 0:gb - ga], T.Sb[:, base + ga:base + gb], 0.0, A.mult, A.max, ["msk", (S, ga, gb)], [("Gb", ga, gb)])
+        def tensor(a, b, md):
+            k = banks[0] % 4
+            banks[0] += 1
+            P = ("PA", "PB")[k // 2]
+            d = T[P][:, 512 * (k % 2):512 * (k % 2) + b - a]
+            s = T[S][:, base + 3 + a:base + 3 + b]
+            bank = (P, k % 2, k % 2 + 1)
+            mm([(d, T[D2 if md == 2 else I][:, 0:128], s, True, False)], [D2 if md == 2 else I, (S, a + 3, b + 3)], [bank], [k])
+            if md == 2:
+                mm([(d, T[J][:, :], T[M4][:, a:b], False, False)], [J, (M4, a, b)], [bank], [k])
+                mm([(d, T[J][:, :], T[M4][:, a + 3:b + 3], False, True)], [J, (M4, a + 3, b + 3)], [bank], [k])
+            else:
+                mm([(d, T[J][:, :], T[M7][:, a:b], False, True)], [J, (M7, a, b)], [bank], [k])
+            act(T.V[:, a:b], d, [bank], [("V", a, b)], [k], later=not b16)
 
-            def carry():
-                mm([(T[P][:, a:b], T.Ib[:, :], T.Gb[:, ga + a:ga + b], True, True) for a, b in ((0, 512), (512, gb - ga))], ["Ib", ("Gb", ga, gb)], [P], Xb)
-            later.append(carry)
-        if side is None:
-            return og, oh, ow, ov
-        Wm, I, J = (side, "Ib", "Jb") if S == "Sb" else (side, "Iw", "Jf")
+        def rest():
+            md, cols = mode
+            mid = min(an + cols, bn)
+            if mid < bn:
+                m7(mid, bn)
+                diff(mid, bn)
 
-        def ow2():
-            vtt(T[Wm][:, 0:nb_ - n1], T[H][:, n1:nb_], T[P][:, n1 + 6 - ga:nb_ + 6 - ga], A.max, [(H, n1, nb_), P], [Wm], Xb)
+        def out():
+            md, cols = mode
+            mid = min(an + cols, bn)
+            if md == 3 and mid > an:
+                m7(an, mid)
+            n = (mid - an + CHUNK - 1) // CHUNK
+            for i in range(n):
+                tensor(an + (mid - an) * i // n, an + (mid - an) * (i + 1) // n, md)
+        return m2, m4, rest, out
 
-        def ov2():
-            mid = (n1 + nb_) // 2
-            for k, (a, b) in enumerate(((n1, mid), (mid, nb_))):
-                d = T.PB[:, 512 * k:512 * k + b - a]
-                mm([(d, T[I][:, 0:128], T[S][:, base + 3 + a:base + 3 + b], True, False), (d, T[J][:, :], T[Wm][:, a - n1:b - n1], False, True)],
-                   [I, J, (S, a + 3, b + 3), Wm], [("PB", k, k + 1)], [2 + k])
-                op("s", lambda e, a=a, b=b, d=d: e.activation(T.V[:, a:b], d, F.Relu, bias=1.0, scale=2.0 ** 32), [("PB", k, k + 1)], [("V", a, b)], [2 + k])
-        return og, oh, ow2, ov2
+    def votes32(S, ja, jb, na, on_tensor):
+        base, nb, hb = FP - 3, min(jb - 6, X + 9 if ja < X else W), X + 9 if ja < X + 9 < jb else jb
+        pre = T.PA[:, 512 + na + 6 - ja:512 + nb + 6 - ja]
+        vscan(T.H[:, hb - 1:ja - 1 if ja else None:-1], T.PA[:, 0:hb - ja], T[S][:, base + hb - 1:base + ja - 1:-1], 0.0, A.mult, A.max,
+              ["msk", (S, ja, hb)], [("H", ja, hb)], [0])
+        vscan(T.PA[:, 512:512 + jb - ja], T.PA[:, 0:jb - ja], T[S][:, base + ja:base + jb], 0.0, A.mult, A.max, ["msk", (S, ja, jb)], [("PA", 1, 2)], [0, 1])
+        s = T[S][:, base + 3 + na:base + 3 + nb]
+        if not on_tensor:
+            vtt(pre, T.H[:, na:nb], pre, A.max, [("H", na, nb), ("PA", 1, 2)], [("PA", 1, 2)], [1])
+            vtt(T.V[:, na:nb], s, pre, A.subtract, [(S, na + 3, nb + 3), ("PA", 1, 2)], [("V", na, nb)], [1])
+            return
+        vtt(T.M[:, na:nb], T.H[:, na:nb], pre, A.max, [("H", na, nb), ("PA", 1, 2)], [("M", na, nb)], [1])
+        k = banks[0] % 2
+        banks[0] += 1
+        d = T.PB[:, 512 * k:512 * k + nb - na]
+        mm([(d, T.Iw[:, 0:128], s, True, False)], [("Iw", 0, 1), (S, na + 3, nb + 3)], [("PB", k, k + 1)], [2 + k])
+        mm([(d, T.Jf[:, :], T.M[:, na:nb], False, True)], ["Jf", ("M", na, nb)], [("PB", k, k + 1)], [2 + k])
+        act(T.V[:, na:nb], d, [("PB", k, k + 1)], [("V", na, nb)], [2 + k])
 
-    v0 = [vote_ops("Sb", 770 * c, 770 * c + 770, 770 * c, 770 * c + 770, max(770 * c - 6, 0), min(770 * c + 764, W), "PA", ("Wb0", "Wb1", "Wb0", None)[c])
-          for c in range(4)]
-    v0[0][0](); later[0](); v0[0][1]()
-    lists(0)
-    keys(0, 0)
-    v0[1][0](); v0[0][2](); later[1](); v0[0][3]()
-    v0[1][1](); v0[2][0]()
-    vcopy(T.Rhi[:, :], T.roti[:, :], ["roti"], ["Rhi"])
-    v0[1][2](); later[2](); v0[1][3]()
-    vtt(T.Rlo[:, :], T.roti[:, :], T.Rhi[:, :], A.subtract, ["roti", "Rhi"], ["Rlo"])
-    dmas("y", "rw", [(T.Rw[0:128:16, :], T.Rhi[:, :]), (T.Rw[4:128:16, :], T.Rlo[:, :])], ["Rhi", "Rlo"], ["Rw"])
-    vcopy(T.hpf[0:8, 0:3], T.hpi[0:8, 0:3], ["hpi"], ["hpf"])
-    v0[2][1](); v0[3][0]()
-    v0[2][2](); later[3](); v0[2][3]()
-    mm([(T.X0[:, 0:3], T.Ew[0:8, sh:sh + 128], T.hpf[0:8, 0:3], True, True),
-        (T.X0[:, 3:5], T.Ew[0:8, 0:128], T.g8[0:8, :], True, True)], ["Ew", "hpf", "g8"], ["X0"], [5])
-    acopy(T.hv[:, 0:5], T.X0[:, 0:5], ["X0"], ["hv"], [5])
-    keys(0, 1, False)
-    v0[3][1]()
-    v0[3][2](); v0[3][3]()
+    v0 = [votes("Sb", (CUT0[c] + 3) * (c > 0), CUT0[c + 1] + (3 if c < 3 else 6), MODE0[c]) for c in range(4)]
+    for v in v0[:3]:
+        for k in (0, 1, 3, 2):
+            v[k]()
+    vcopy(T.Qf[:, :], T.roti[:, :], ["roti"], ["Qf"])
+    rows("", "Rw", "X1")
+    v0[3][0](); v0[3][1](); v0[3][3]()
+    targets(0); keys(0, 0, "X2")
+    offsets(0)
+    v0[3][2](); keys_out(0, "X2"); keys(0, 1, "X2")
 
     for t in range(FR):
         last = t == FR - 1
@@ -350,155 +476,191 @@ def rank_program(g, core, T, topo):
         Tl = "T0" if t == 0 else "T1"
         Tt = ("T0", "T1", "T2")[t]
         Ts, Qu = "Ts%d" % t, "Qu%d" % t
-        turn = 16 * (FR - 1 - t)
+        turn = -16 * t % 128
+        table, tk = T.C2[:, :], "C2"
 
+        mm([(T.D[0:96, :], T.ob[0:1, 0:96], T.brow[0:1, :], True, False)], ["ob", "brow"], ["D"], [4])
         for u in range(2):
             for h, q in enumerate("vs"):
                 o = T.G[:, 1568 * u + 16 + 768 * h:1568 * u + 16 + 768 * h + 768]
                 w = T.V[:, :].indirect(T.Lit[:, u, 96 * t + 48 * h:96 * t + 48 * h + 48])
                 R, Wr = ["V", ("Lit", 2 * t + u, 2 * t + u + 1)], [("G", 2 * u + h, 2 * u + h + 1)]
                 if q == "v":
-                    vts(o, w, VS, VB, A.mult, A.add, R, Wr)
+                    vts(o, w, 0.0, 64.0, A.is_ge, A.mult, R, Wr, rate=GATHER)
                 else:
-                    op("s", lambda e, o=o, w=w: e.activation(o, w, F.Identity, bias=VB, scale=VS), R, Wr)
+                    act(o, w, R, Wr, fn=F.Relu, rate=GATHER, bias=64.0, scale=2.0 ** 38)
             lst = []
             for j, (uu, s) in enumerate(PIECES):
                 if uu == u:
                     for r in range(16):
                         a = 1568 * u + 16 * (1 + s) + r
-                        lst.append((T.D[0:96, 16 * j + r:512:64], T.G[:, a:a + 16 * 95 + 1:16], T.ind[:, :], True, True))
+                        lst.append((T.D[0:96, 16 * j + r:512:64], T.G[:, a:a + 16 * 95 + 1:16], T.ind[:, :], False, u == 1 and j == 2 and r == 15))
             mm(lst, [("G", 2 * u, 2 * u + 2), ("G", 10, 14), "ind"], ["D"], [4])
         if t == 0:
-            keys_out(1)
-            zero("Rr", range(2, 3))
-            vts(T.Lm[:, :], T.Lf[:, :], T.hv[:, 3:4], None, A.subtract, None, ["Lf", "hv"], ["Lm"])
+            keys_out(1, "X2")
+            vcopy(T.hpf[0:8, 0:3], T.hpi[0:8, 0:3], ["hpi"], ["hpf"])
+            act(T.C2[:, 2 * WC:], T.C2[:, 0:16], [("C2", 0, 16)], [("C2", 2 * WC, 2 * WC + 16)])
+            mm([(T.X0[:, 0:3], T.Ew[0:8, 0:128], T.hpf[0:8, 0:3], True, True),
+                (T.X0[:, 3:5], T.Ew[0:8, 0:128], T.g8[0:8, :], True, True)], ["Ew", "hpf", "g8"], ["X0"], [5])
+            act(T.hv[:, 0:5], T.X0[:, 0:5], ["X0"], [("hv", 0, 5)], [5])
+            vts(T.Lm[:, :], T.Lf[:, :], T.hv[:, 3:4], None, A.add, None, ["Lf", ("hv", 0, 5)], ["Lm"])
         else:
-            window(range(W1, W2))
+            window(range(WG, 16))
+            if not last:
+                offsets(t + 1)
         if not last:
-            lists(t + 1)
+            targets(t + 1)
         vscan(T.LF[0:96, 0:496], T.D[0:96, 0:496], T.KF[0:96, 0:496], HUGE, A.min, A.max, ["D", "KF"], [("LF", 0, 1)], [4])
-        vscan(T.LB[0:96, rev(16, 512)], T.D[0:96, rev(16, 512)], T.KB[0:96, rev(16, 512)], HUGE, A.min, A.max, ["D", "KB"], [("LB", 0, 1)], [4])
-        acopy(T.MF[:, :], T.LF[:, 16:496].indirect(T.Lm[:, :]), ["LF", "Lm"], ["MF"])
-        mm([(T.X0[:, u:192:2], T.MF[0:97, 128 * u:128 * u + 128], T.I97[0:97, :], True, True) for u in range(2)], ["MF", "I97"], ["X0"], [5])
-        vcopy(T.MB[:, :], T.LB[:, 16:512].indirect(T.Lm[:, :]), ["LB", "Lm"], ["MB"])
-        mm([(T.X1[:, u:192:2], T.MB[0:97, 128 * u:128 * u + 128], T.I97[0:97, :], True, True) for u in range(2)], ["MB", "I97"], ["X1"], [6])
-        F2, sg, sd, sr = T.PA[:, 0:192], T.PA[:, 192:384], T.PA[:, 512:704], T.PA[:, 704:896]
-        vscan(F2, T.c17[:, :], T.X0[:, 0:192], HUGE, A.add, A.min, ["c17", "X0"], [("PA", 0, 1)], [0, 5])
+        vscan(T.LB[0:96, 511:15:-1], T.D[0:96, 511:15:-1], T.KB[0:96, 511:15:-1], HUGE, A.min, A.max, ["D", "KB"], [("LB", 0, 1)], [4])
+        for L, M, B in (("LF", "MF", "X0"), ("LB", "MB", "X1")):
+            for u in range(2):
+                (vcopy if L == "LF" and u < MV else act)(T[M][:, u, :], T[L][:, 16:496].indirect(T.Lm[:, 8 * u:8 * u + 8]), [L, "Lm"], [(M, u, u + 1)], rate=GATHER)
+                mm([(T[B][:, u:192:2], T[M][0:97, u, :], T.I97[0:97, :], True, True)], [(M, u, u + 1), "I97"], [B], [XB[B]])
+        if t == 0:
+            act(T.hv[:, 5:8], T.hv[:, 0:3], [("hv", 0, 5)], [("hv", 5, 8)], scale=2.0 ** -11)
+            act(T.mc[:, :], T.mp[:, :], ["mp", ("hv", 0, 5)], ["mc"], fn=F.Identity, bias=T.hv[:, 3:4])
+            for c in range(4):
+                act(T.Rr[:, X * c:X * c + X], T.G[:, 0:X], ["G"], [("Rr", c, c + 1)], scale=0.0, later=True)
+            act(T.Jf[:, :], T.Iw[:, 0:128], [("Iw", 0, 1)], ["Jf"], scale=-1.0)
+            act(T.Kw[:, :], T.Iw[:, :], ["Iw"], ["Kw"], scale=-2048.0)
+            act(T.Df[:, :], T.Iw[:, 0:128], [("Iw", 0, 1)], ["Df"], scale=2.0)
+        act(T.Hd[:, t, 0:128 + turn], T.Iw[:, 0:128 + turn], ["Iw", ("hv", 0, 5)], [("Hd", t, t + 1)], fn=F.Identity, scale=T.hv[:, t:t + 1])
+        if not last:
+            keys(t + 1, 0, "X2")
+        vscan(T.PA[:, 704:896], T.c17[:, :], T.X0[:, 0:192], HUGE, A.add, A.min, ["c17", "X0"], [("PA", 1, 2)], [1, 5])
+        if t == 0 and not PAIRS:
+            vmem(T.PA[:, 0:511], 1.0, [("PA", 0, 1), "msk"], [0])
+            vmem(T.PA[:, 0:511:7], 0.0, [("PA", 0, 1), "msk"], [0])
+        if t == 0:
+            offsets(1)
         vscan(T.B2[:, ::-1], T.c17[:, :], T.X1[:, 191::-1], HUGE, A.add, A.min, ["c17", "X1"], ["B2"], [6])
-        sg = T.PB[:, 0:192]
-        vtt(T.Dd[:, :], T.B2[:, :], F2, A.subtract, ["B2", ("PA", 0, 1)], ["Dd"], [0])
-        vtt(T.Wi[:, :], T.B2[:, :], F2, A.min, ["B2", ("PA", 0, 1)], ["Wi"], [0])
-        op("s", lambda e, sg=sg: e.activation(sg, T.Dd[:, :], F.Sign), ["Dd"], ["PB"], [2])
-        if t > 0:
-            window(range(W2, 16))
-        else:
-            zero("Rr", range(3, 4))
-        vts(T.di[:, :], T.Wi[:, :], 2.0 ** -13, -C0 / 8192 - 0.4375, A.mult, A.add, ["Wi"], ["di"])
-        vts(T.pi[:, :], T.Wi[:, :], 4095, None, A.bitwise_and, None, ["Wi"], ["pi"])
-        vtt(sd, T.di[:, :], sg, A.mult, ["di", "PB"], [("PA", 2, 3)], [2, 1])
-        vtt(sr, T.pi[:, :], sd, A.add, ["pi", ("PA", 2, 3)], [("PA", 3, 4)], [1])
-        vts(T.Ls[:, :], sr, 0.0, float(W - 1), A.max, A.min, [("PA", 3, 4)], ["Ls"], [1])
-        vtt(T.dm[:, :], T.mc[:, :], sr, A.subtract, ["mc", ("PA", 3, 4)], ["dm"], [1])
 
-        def e_ops():
-            vts(T.ei[:, :], T.dm[:, :], T.hv[:, 3:4], T.hv[:, t:t + 1], A.subtract, A.mult, ["dm", "hv"], ["ei"])
-            vts(T.em[:, :], T.ei[:, :], WC - 1, None, A.bitwise_and, None, ["ei"], ["em"])
-            vcopy(T.ef[:, :], T.em[:, :], ["em"], ["ef"])
+        def sources(parts):
+            steps = []
+            for k, (a, b) in enumerate(parts):
+                c = slice(a, b)
+                F2, sd, sg = T.PA[:, 704 + a:704 + b], T.PA[:, 512 + a:512 + b], T.PB[:, 512 * k + a:512 * k + b]
+                pa = ("sd", a, b)
+                steps.append([
+                    lambda c=c, F2=F2, a=a, b=b: vtt(T.Dd[:, c], T.B2[:, c], F2, A.subtract, ["B2", ("PA", 1, 2)], [("Dd", a, b)], [1]),
+                    lambda c=c, F2=F2, a=a, b=b: vtt(T.Wi[:, c], T.B2[:, c], F2, A.min, ["B2", ("PA", 1, 2)], [("Wi", a, b)], [1]),
+                    lambda c=c, sg=sg, a=a, b=b, k=k: act(sg, T.Dd[:, c], [("Dd", a, b)], [("PB", k, k + 1)], [2 + k], fn=F.Sign),
+                    lambda c=c, a=a, b=b: vts(T.di[:, c], T.Wi[:, c], 2.0 ** -13, -C0 / 8192 - 0.4375, A.mult, A.add, [("Wi", a, b)], [("di", a, b)]),
+                    lambda c=c, a=a, b=b: vts(T.pi[:, c], T.Wi[:, c], 4095, None, A.bitwise_and, None, [("Wi", a, b)], [("pi", a, b)]),
+                    lambda c=c, sd=sd, sg=sg, a=a, b=b, k=k, pa=pa: vtt(sd, T.di[:, c], sg, A.mult, [("di", a, b), ("PB", k, k + 1), ("PA", 1, 2)], [pa], [2 + k, 1]),
+                    lambda c=c, sd=sd, a=a, b=b, pa=pa: vtt(sd, T.pi[:, c], sd, A.add, [("pi", a, b), pa, ("PA", 1, 2)], [pa], [1]),
+                    lambda c=c, sd=sd, a=a, b=b, pa=pa: vts(T.Ls[:, c], sd, 0.0, float(W - 1), A.max, A.min, [pa, ("PA", 1, 2)], [("Ls", a, b)], [1], rate=1.0),
+                    lambda c=c, sd=sd, a=a, b=b, pa=pa: vtt(T.dm[:, c], T.mc[:, c], sd, A.subtract, ["mc", pa, ("PA", 1, 2)], [("dm", a, b)], [1]),
+                    lambda c=c, a=a, b=b: affine(EQ[last], T.a2[:, c], T.dm[:, c], T.hv[:, 5 + t:6 + t], MAGIC, [("dm", a, b), ("hv", 5, 8)], [("a2", a, b)])])
+            return steps
 
         def gb(c):
             a, b = c
-            acopy(T.Rg[:, 16 * a:16 * b], T.Rw[:, :].indirect(T.Ls[:, a:b]), ["Rw", "Ls"], [("Rg", a, b)])
+            act(T.Rg[:, 16 * a:16 * b], T.Rw[:, :].indirect(T.Ls[:, a:b]), ["Rw", ("Ls", a, b)], [("Rg", a, b)], rate=GATHER)
 
-        def gc(c, q):
+        def gc(c, q, small=0):
             a, b = c
+            w, R = T[So][:, so:so + W].indirect(T.Ls[:, a:b]), [So, ("Ls", a, b)]
             if a >= 144:
                 o, Wr = T[Ts][:, 16 * a - 2304:16 * b - 2304], [(Ts, a, b)]
             else:
                 o, Wr = T[Tl][:, X + 16 * a:X + 16 * b], [(Tl, X + 16 * a, X + 16 * b)]
-            (vcopy if q == "v" else acopy)(o, T[So][:, so:so + W].indirect(T.Ls[:, a:b]), [So, "Ls"], Wr)
+            k = 2.0 ** -10 if small else 1.0
+            if q == "v":
+                vts(o, w, k, None, A.mult, None, R, Wr, rate=GATHER)
+            else:
+                act(o, w, R, Wr, rate=GATHER, scale=k)
 
         def ext(c, B):
             a, b = c
             o = turn if a >= 144 else 0
-            lst = [(T[B][:, 0:b - a], T.Z[:, 15 - r + o:143 - r + o], T.Rg[:, 16 * a + r:16 * b:16], r == 0, False) for r in range(16)]
+            mm([(T[B][:, 0:b - a], T.Kw[:, o:o + 128], T.a2[:, a:b], True, False), (T[B][:, 0:b - a], T.ob[0:1, :], T.krow[0:1, 0:b - a], False, False),
+                (T[B][:, 0:b - a], T.Hd[:, t, o:o + 128], T.dm[:, a:b], False, False)],
+               ["Kw", "ob", "krow", ("Hd", t, t + 1), ("dm", a, b), ("a2", a, b)], [B], [XB[B]])
+            lst = [(T[B][:, 0:b - a], T.Z[:, 15 - r + o:143 - r + o], T.Rg[:, 16 * a + r:16 * b:16], False, r == 15) for r in range(16)]
             mm(lst, ["Z", ("Rg", a, b)], [B], [XB[B]])
-            mm([(T[B][:, 0:b - a], T.Iw[:, o:o + 128], T.ef[:, a:b], False, True)], ["Iw", "ef"], [B], [XB[B]])
 
         def qq(c, B):
             a, b = c
             if a >= 144:
-                vcopy(T.Qs[:, 48 * t:48 * t + 48], T[B][:, 0:48], [B], [("Qs", t, t + 1)], [XB[B]])
+                vts(T.Qs[:, 48 * t:48 * t + 48], T[B][:, 0:48], float(WC), None, A.add, None, [B], [("Qs", t, t + 1)], [XB[B]])
                 send(T[Qu][:, 0:48], T.Qs[:, 48 * t:48 * t + 48], "aQ%d" % t, [("Qs", t, t + 1)])
             else:
-                vcopy(T[Qu][:, 48 + a:48 + b], T[B][:, 0:b - a], [B], [(Qu, 48 + a, 48 + b)], [XB[B]])
+                vts(T[Qu][:, 48 + a:48 + b], T[B][:, 0:b - a], float(WC), None, A.add, None, [B], [(Qu, 48 + a, 48 + b)], [XB[B]])
 
-        def gd(a, b):
+        def gd(a, b, small=0):
             src, nm = (T[Tt][:, a:b], Tt) if a < X else (T[Tl][:, a:b], Tl)
-            vtt(T[Sn][:, FP + a:FP + b], T.C2[:, :].indirect(T[Qu][:, a // 16:b // 16]), src, A.mult,
-                ["C2", (Qu, a // 16, b // 16), (nm, a, b)], [(Sn, 3 + a, 3 + b)])
+            w, R = table.indirect(T[Qu][:, a // 16:b // 16]), [tk, (Qu, a // 16, b // 16)]
+            if small:
+                act(T.Cg[:, a:b], w, R, [("Cg", a, b)], rate=GATHER, scale=1024.0)
+                B = "X1" if b == X else "X0"
+                mm([(T[B][:, 0:b - a], T.Iw[:, turn:turn + 128], T[Tt][:, a:b], True, True)], ["Iw", (Tt, a, b)], [B], [XB[B]])
+                vscan(T[Sn][:, FP + a:FP + b], T.Cg[:, a:b], T[B][:, 0:b - a], 0.0, A.max, A.mult, [("Cg", a, b), B], [(Sn, 3 + a, 3 + b)], [XB[B]])
+            else:
+                vtt(T[Sn][:, FP + a:FP + b], w, src, A.mult, R + [(nm, a, b)], [(Sn, 3 + a, 3 + b)], rate=GATHER)
+
+        def pass_on(a, b, i, q, small=0):
+            c = (144 + a // 16, 144 + b // 16)
+            gc(c, q, small)
+            send(T[Tt][:, a:b], T[Ts][:, a:b], "aT%d%d" % (t, i), [(Ts,) + c])
+            arrive("aT%d%d" % (t, i), [(Tt, a, b)])
 
         top = (144, 192)
         arrive("aQ%d" % t, [(Qu, 0, 48)])
         if not last:
-            c0, c1, c2 = (0, K1), (K1, K2), (K2, 144)
-            n1, n2 = X + 16 * K1, X + 16 * K2
-            j1, j2 = (n1 + 3) // 7 * 7, (n2 + 3) // 7 * 7
-            L, halves = "L%d" % t, t + 1
-            wide = X // halves
-            for i in range(halves):
-                arrive("aT%d%d" % (t, i), [(L, i, i + 1)])
-                dmas("y", "lT%d%d" % (t, i), [(T[Tt][p, wide * i:wide * i + wide], T[L][i, r, :]) for p, r in turned(turn)],
-                     [(L, i, i + 1)], [(Tt, wide * i, wide * i + wide)])
-            P = (("PB", "PA", "PB", "PA"), ("PA", "PA", "PB", "PA"), ("PA", "PA", "PA", "PB"), ("PA", "PA", "PA", "PA"))[PE]
-            side = [("Wf0", "Wf1", "Wf0")[i] if i < PE else None for i in range(3)]
-            va = [vote_ops(Sn, 777, j1, 777, j1, 777, j1 - 6, P[0], side[0]), vote_ops(Sn, j1, j2, j1, j2, j1 - 6, j2 - 6, P[1], side[1]),
-                  vote_ops(Sn, j2, 3080, j2, 3080, j2 - 6, W, P[2], side[2]), vote_ops(Sn, 0, 784, 0, 777, 0, 777, P[3])]
-            gb(c0); e_ops(); gc(c0, CQ); ext(c0, "X0")
-            for i in range(halves):
-                c = (144 + wide * i // 16, 144 + wide * (i + 1) // 16)
-                gc(c, "s")
-                send(T[L][i], T[Ts][:, wide * i:wide * i + wide], "aT%d%d" % (t, i), [(Ts,) + c])
-            qq(c0, "X0"); gd(X, n1)
-            keys(t + 1, 0, False)
-            gb(c1); ext(c1, "X1"); gc(c1, "s"); va[0][0](); va[0][1]()
-            gb(top); ext(top, "X0")
-            qq(c1, "X1"); gd(n1, n2); va[0][2](); qq(top, "X0")
-            gb(c2); ext(c2, "X1"); gc(c2, "s"); keys_out(0)
-            va[1][1]()
-            if PE:
-                va[0][3](); va[1][0]()
+            cs = list(zip(CUT[:-1], CUT[1:]))
+            n = [X + 16 * k for k in CUT]
+            if PAIRS:
+                va = [votes(Sn, n[i] + 3, n[i + 1] + (3 if i + 1 < len(cs) else 6), PMODE[i]) for i in range(len(cs))]
+                va += [votes(Sn, 0, X + 3, PMODE[-1], True)] if PAIRS == 1 else [votes(Sn, 0, 390, PMODE[-1]), votes(Sn, 390, X + 3, PMODE[-1], True)]
+            done = [X + 9, 0]
+
+            def vote_to(j, start):
+                parts = (j - done[0] + SPAN - 1) // SPAN
+                for k in range(parts):
+                    a = done[0]
+                    b = a + (j - a) // 7 // (parts - k) * 7
+                    votes32(Sn, a, b, max(a - 6, start), MODE[done[1]] == "t")
+                    done[:] = [b, done[1] + 1]
+
+            for fs in zip(*sources([(0, HEAD), (HEAD, 192)] if HEAD else [(0, 192)])):
+                for f in fs:
+                    f()
+            keys_out(0, "X2"); keys(t + 1, 1, "X2")
+            gb(cs[0])
+            for i, c in enumerate(cs):
+                if i:
+                    gb(c)
+                ext(c, "X%d" % (i % 2)); gc(c, GC[i])
+                if i == TOP_T:
+                    for k in range(t + 1):
+                        pass_on(X * k // (t + 1), X * (k + 1) // (t + 1), k, GC[-1], t)
+                qq(c, "X%d" % (i % 2))
+                if i == TOP_Q:
+                    gb(top); ext(top, "D"); qq(top, "D")
+                if i + 1 == len(cs):
+                    vcopy(T.Qf[:, :], T[Qu][:, :], [Qu], ["Qf"])
+                    rows(t, "Rr", "D")
+                gd(n[i], n[i + 1])
+                if PAIRS:
+                    va[i][0](); va[i][1]()
+                else:
+                    vote_to((n[i + 1] + 3) // 7 * 7 if i + 1 < len(cs) else 3080, X + 9)
+            keys_out(1, "X2")
+            done[0] = 0
+            if PAIRS:
+                for k in range(t + 1):
+                    gd(X * k // (t + 1), X * (k + 1) // (t + 1), t)
+                for v in va[:len(cs)]:
+                    v[3](); v[2]()
+                for k in (0, 1, 3, 2):
+                    for v in va[len(cs):]:
+                        v[k]()
             else:
-                va[1][0](); va[0][3]()
-            qq(c2, "X1"); gd(n2, W)
-            keys(t + 1, 1, False)
-            if RE:
-                va[1][2]()
-            vcopy(T.Qf[:, :], T[Qu][:, :], [Qu], ["Qf"])
-            vts(T.Rge[:, :], T[Qu][:, :], float(WC), -float(WC), A.is_ge, A.mult, [Qu], ["Rge"])
-            acopy(T.Rhi[:, :], T.Qf[:, :], ["Qf"], ["Rhi"])
-            keys_out(1)
-            if RE:
-                va[2][1]()
-            else:
-                va[1][2]()
-            vtt(T.Rlo[:, :], T.Qf[:, :], T.Rhi[:, :], A.subtract, ["Qf", "Rhi"], ["Rlo"])
-            rows(t)
-            if PE >= 2:
-                va[1][3]()
-            if not RE:
-                va[2][1]()
-            va[2][0]()
-            if PE < 2:
-                va[1][3]()
-            va[2][2]()
-            if PE == 3:
-                window(range(W0))
-                va[2][3](); gd(0, X)
-                window(range(W0, W1))
-            else:
-                window(range(W1))
-                gd(0, X); va[2][3]()
-            va[3][0](); va[3][1](); va[3][2](); va[3][3]()
+                for k in range(2):
+                    gd(X // 2 * k, X // 2 * (k + 1), t)
+                    vote_to((385, X + 16)[k], 1)
+            window(range(WG))
         else:
             acc = T.PB
 
@@ -506,38 +668,35 @@ def rank_program(g, core, T, topo):
                 lst = []
                 for i, (a, b) in enumerate(parts):
                     lst.append((acc[:, a % 512:a % 512 + b - a], T.Iw[:, 0:128], T[Sn][:, FP + a:FP + b], start and i == 0, stop and i == len(parts) - 1))
-                mm(lst, ["Iw"] + [(Sn, 3 + a, 3 + b) for a, b in parts], ["PB"], [2])
+                mm(lst, ["Iw"] + [(Sn, 3 + a, 3 + b) for a, b in parts], ["acc", ("PB", 0, 1)], [2])
 
             def store(h):
                 a, b = 256 * h, 256 * h + 256
-                vtt(T.Y[:, a:b], T[Sn][:, FP + a:FP + b], acc[:, a:b], A.add, [(Sn, 3 + a, 3 + b), ("PB", h, h + 1)], [("Y", h, h + 1)], [2])
-                dmas("ys"[h], "y%d" % h, [(T.y[r, a:b], T.Y[p, a:b]) for p, r in lay], [("Y", h, h + 1)], [("out", h, h + 1)])
+                vtt(T.Y[:, a:b], T[Sn][:, FP + a:FP + b], acc[:, a:b], A.add, [(Sn, 3 + a, 3 + b), ("acc", a, b)], [("Y", h, h + 1)], [2])
+                dmas("ys"[h], "y%d" % h, [(T.y[:, a:b], T.Y[:, a:b])], [("Y", h, h + 1)], [("out", h, h + 1)])
 
-            c0, c1, c2 = (0, 48), (48, 96), (96, 144)
-            for i, (a, b) in enumerate(((256, X), (0, 256))):
-                gc((144 + a // 16, 144 + b // 16), "s")
-                send(T.T2[:, a:b], T.Ts2[:, a:b], "aT2%d" % i, [(Ts, 144 + a // 16, 144 + b // 16)])
-                arrive("aT2%d" % i, [("T2", a, b)])
-            e_ops(); gb(top); gc(c0, "v"); ext(top, "X0"); gb(c0); gc(c1, "v"); ext(c0, "X1"); qq(top, "X0")
-            gb(c1)
-            if K3 > 96:
-                gc((96, K3), "v")
+            c0, c1, c2 = zip(CUTL[:-1], CUTL[1:])
+            for fs in zip(*sources([(144, 192), (0, 144)] if HEAD else [(0, 192)])):
+                for f in fs:
+                    f()
+
+            def add(a, b):
+                o = acc[:, a % 512:a % 512 + b - a]
+                vtt(o, T[Sn][:, FP + a:FP + b], o, A.add, [(Sn, 3 + a, 3 + b)], [("acc", a % 512, a % 512 + b - a)], [2])
+
+            pass_on(256, X, 0, "v", 1); gb(top); pass_on(0, 256, 1, "v", 1)
+            ext(top, "D"); gb(c0); gc(c0, "v"); qq(top, "D"); ext(c0, "X1")
+            gb(c1); gc((48, K3), "v")
             ext(c1, "X0"); qq(c0, "X1"); gd(1024, 2 * X); fold([(1024, 1536)], True, False); gd(X, 1024)
-            gb(c2); ext(c2, "X1")
-            if K3 < 144:
-                gc((K3, 144), "s")
-            fold([(768, 1024)], False, False)
-            if FO == 0:
-                qq(c1, "X0"); gd(2 * X, 2048); fold([(1536, 2048)], False, False); gd(2048, 3 * X); fold([(2048, 2304)], False, False)
-                qq(c2, "X1"); gd(3 * X, 2560); fold([(2304, 2560)], False, True); gd(2560, W)
-            else:
-                qq(c1, "X0"); gd(2 * X, 2048); fold([(1536, 2048)], False, True); qq(c2, "X1"); gd(2048, W)
-                vtt(acc[:, 0:512], T[Sn][:, FP + 2048:FP + 2560], acc[:, 0:512], A.add, [(Sn, 2051, 2563), "PB"], ["PB"], [2])
-            gd(256, X)
-            vtt(acc[:, 0:512], T[Sn][:, FP + 2560:FP + W], acc[:, 0:512], A.add, [(Sn, 2563, 3 + W), "PB"], ["PB"], [2])
-            gd(0, 256)
-            store(1)
-            vtt(acc[:, 0:256], T[Sn][:, FP + 512:FP + X], acc[:, 0:256], A.add, [(Sn, 515, 3 + X), ("PB", 0, 1)], [("PB", 0, 1)], [2])
-            store(0)
+            gb(c2); ext(c2, "X1"); gc((K3, 144), "s")
+            fold([(768, 1024)], False, FOLD == 0)
+            qq(c1, "X0"); gd(2 * X, 3 * X)
+            for k, (a, b) in enumerate(((1536, 2048), (2048, 2304))):
+                if k < FOLD:
+                    fold([(a, b)], False, k + 1 == FOLD)
+                else:
+                    add(a, b)
+            qq(c2, "X1"); gd(3 * X, W); add(3 * X, 2560); add(2560, 2816); add(2816, W)
+            gd(256, X, 1); store(1); gd(0, 256, 1); add(512, X); store(0)
     op("g", lambda e: e.wait_ge(T.sem.sent, sends[0]), ["out"])
-    emit(g, T, ops)
+    emit(g, T, arrange(ops))

import math

from concourse.mybir import AluOpType as A, ActivationFunctionType as F

W, WC, FR, X = 3072, 2048, 3, 768
HUGE = float(2 ** 26)
BIG = 2 ** 23
C0 = -(2 ** 24) + 2 ** 18
MAGIC = 1.5 * 2 ** 23
FP, BP = 8, 16

CUT0 = (0, 768, 1536, 2304, W)
MODE0 = ((2, W), (2, W), (2, 384), (2, 0))
CUT = (0, 24, 64, 104, 144)
MODE, SPAN = "ttttttvv", 511
GC = "vssv" + "v"
TOP_T, TOP_Q, WG, CHUNK = 0, 1, 8, 512
CUTL = (0, 48, 96, 144)
K3, EQ = 96, "vs"

CYCLE, PE_CYCLE, GATHER, HOP, LOCAL, LINK = 0.00083, 0.00043, 1.4, 0.12, 300e3, 70e3
ROUNDS, ISSUE, FOLD, REMOTE, ROWS, OWN = 2, 0.2, 1, 2.5, 4.0, 0.4
SLACKS, MV, HEAD = (0.0, 0.1, 0.2, 0.36), 0, 48
PAIRS, PMODE = 2, ((2, W), (2, W), (2, W), (2, 0), (2, 0))

f32, bf, i32, u16 = "float32", "bfloat16", "int32", "uint16"
SCRATCH = {
    "Sb": ("sbuf", [128, W + 2 * BP], bf), "S1": ("sbuf", [128, W + 2 * FP], f32), "S2": ("sbuf", [128, W + 2 * FP], f32),
    "T0": ("sbuf", [128, W], bf), "T1": ("sbuf", [128, W], f32), "T2": ("sbuf", [128, X], f32),
    "Ts0": ("sbuf", [128, X], bf), "Ts1": ("sbuf", [128, X], f32), "Ts2": ("sbuf", [128, X], f32),
    "Qu0": ("sbuf", [128, 192], u16), "Qu1": ("sbuf", [128, 192], u16), "Qu2": ("sbuf", [128, 192], u16),
    "Qs": ("sbuf", [128, 144], u16),
    "C2": ("sbuf", [128, 2 * WC + 16], bf), "Rw": ("sbuf", [128, W], bf), "Rg": ("sbuf", [128, W], bf),
    "V": ("sbuf", [128, W], bf), "Cg": ("sbuf", [128, W], bf), "G": ("sbuf", [128, 2 * 98 * 16], bf),
    "H": ("sbuf", [128, 3080], f32), "M": ("sbuf", [128, 3080], f32),
    "M2": ("sbuf", [128, 3080], f32), "M4": ("sbuf", [128, 3080], f32), "M7": ("sbuf", [128, 3080], f32),
    "N2": ("sbuf", [128, 3080], bf), "N4": ("sbuf", [128, 3080], bf), "N7": ("sbuf", [128, 3080], bf),
    "iti": ("sbuf", [128, 576], i32), "Lit": ("sbuf", [128, 2, 288], u16), "itf": ("sbuf", [128, 2, 290], f32),
    "roti": ("sbuf", [128, 192], i32), "hpi": ("sbuf", [128, 4], i32), "hpf": ("sbuf", [128, 4], f32),
    "g8": ("sbuf", [128, 2], f32), "hv": ("sbuf", [128, 8], f32), "Hd": ("sbuf", [128, 3, 240], f32),
    "Rhi": ("sbuf", [128, 192], bf), "Rlo": ("sbuf", [128, 192], bf), "Qf": ("sbuf", [128, 192], f32), "Rr": ("sbuf", [128, W], bf),
    "KF": ("sbuf", [128, 512], f32), "KB": ("sbuf", [128, 512], f32),
    "LF": ("sbuf", [128, 512], f32), "LB": ("sbuf", [128, 512], f32), "Lf": ("sbuf", [128, 16], f32), "Lm": ("sbuf", [128, 16], u16),
    "MF": ("sbuf", [128, 2, 128], f32), "MB": ("sbuf", [128, 2, 128], f32),
    "B2": ("sbuf", [128, 192], f32), "Wi": ("sbuf", [128, 192], i32), "Dd": ("sbuf", [128, 192], f32),
    "pi": ("sbuf", [128, 192], i32), "di": ("sbuf", [128, 192], i32), "Ls": ("sbuf", [128, 192], u16),
    "b2": ("sbuf", [128, 192], f32), "Rk": ("sbuf", [128, 192], bf), "dm": ("sbuf", [128, 192], f32), "a2": ("sbuf", [128, 192], f32), "Kw": ("sbuf", [128, 240], f32), "krow": ("sbuf", [128, 64], bf),
    "c17": ("sbuf", [128, 192], f32), "mc": ("sbuf", [128, 192], f32), "mp": ("sbuf", [128, 192], f32),
    "of": ("sbuf", [128, 128], f32), "ob": ("sbuf", [128, 128], bf), "nb": ("sbuf", [128, 8], bf),
    "Iw": ("sbuf", [128, 240], f32), "I97": ("sbuf", [128, 96], f32), "Ew": ("sbuf", [128, 128], f32),
    "ind": ("sbuf", [128, 8], bf), "tm8": ("sbuf", [128, 8], bf),
    "Z": ("sbuf", [128, 256], bf), "crow": ("sbuf", [128, 2, 512], bf), "brow": ("sbuf", [128, 512], bf),
    "Jb": ("sbuf", [128, 128], bf), "Db": ("sbuf", [128, 128], bf),
    "Jf": ("sbuf", [128, 128], f32), "Df": ("sbuf", [128, 128], f32),
    "Y": ("sbuf", [128, 512], f32),
    "PA": ("psum", [128, 1024], f32), "PB": ("psum", [128, 1024], f32), "D": ("psum", [128, 512], f32),
    "X0": ("psum", [128, 512], f32), "X1": ("psum", [128, 512], f32), "X2": ("psum", [128, 8, 64], f32),
}
SEMAPHORES = ["qv", "qs", "qt", "qg", "sent", "sp0", "sp1", "sp2", "sp3", "rec", "itg", "rot", "hop", "rw", "rw0", "rw1",
              "aT00", "aT10", "aT11", "aT20", "aT21", "aQ0", "aQ1", "aQ2", "y0", "y1"]


def meets(a, b):
    return a[0] == b[0] and a[1] < b[2] and b[1] < a[2]


def tok(x):
    return (x, 0, 1 << 30) if isinstance(x, str) else x


def count(ap):
    return math.prod(ap.shape[1:])


def width(name):
    return 2 if name in SCRATCH and SCRATCH[name][2] in (bf, u16) else 4


def size(ap):
    return ap.shape[0] * count(ap) * (width(ap.name) if ap.name in SCRATCH else 4)


def clash(p, o):
    return (any(meets(a, b) for a in p["W"] for b in o["R"] + o["W"]) or any(meets(a, b) for a in p["R"] for b in o["W"])
            or (p["q"] != o["q"] and any(b in p["X"] for b in o["X"])))


def arrange(ops):
    n = len(ops)
    seen, before = {}, []
    for i, o in enumerate(ops):
        names = {a[0] for a in o["R"] + o["W"]} | set(o["X"])
        before.append(sorted(j for j in set().union(*[seen.get(x, ()) for x in names]) if clash(ops[j], o)))
        o["needs"] = [ops[j] for j in before[i]]
        for x in names:
            seen.setdefault(x, []).append(i)
    for i, o in enumerate(ops):
        if o["tag"]:
            k = [j for j, p in enumerate(ops) if p["q"] is None and p["sem"] == o["tag"][0]][0]
            before[k].append(i)
            before[n - 1].append(i)
            ops[k]["busy"] = o["tag"][1]
    after = [[] for o in ops]
    for i in range(n):
        for j in before[i]:
            after[j].append(i)
    def gap(j, i):
        return ops[j]["late"] + (HOP if ops[j]["q"] != ops[i]["q"] else 0.0 if ops[i]["q"] == "t" else OWN)

    def place(key, back):
        pre, post = (after, before) if back else (before, after)
        left = [len(b) for b in pre]
        ready = {i for i in range(n) if not left[i]}
        taken, end = {}, [0.0] * n
        while ready:
            i = min(ready, key=lambda k: (key[k], k))
            ready.remove(i)
            at = max([end[j] + (gap(i, j) if back else gap(j, i)) for j in pre[i]], default=0.0)
            line = taken.setdefault(ops[i]["q"], [])
            k = 0
            while k < len(line) and line[k][0] < at + ops[i]["busy"] - 1e-9:
                at = max(at, line[k][1])
                k += 1
            line.insert(k, (at, at + ops[i]["busy"]))
            end[i] = at + ops[i]["busy"]
            for k in post[i]:
                left[k] -= 1
                if not left[k]:
                    ready.add(k)
        return end

    def run(key, slack, back):
        pre, post = (after, before) if back else (before, after)
        left = [len(b) for b in pre]
        ready = {i: 0.0 for i in range(n) if not left[i]}
        free, end = {}, [0.0] * n
        while ready:
            start = {i: max(r, free.get(ops[i]["q"], 0.0)) for i, r in ready.items()}
            first = min(start, key=lambda i: (start[i], key[i]))
            q = ops[first]["q"]
            i = min((key[k], k) for k in start if ops[k]["q"] == q and start[k] <= start[first] + slack)[1]
            end[i] = free[q] = start[i] + ops[i]["busy"]
            del ready[i]
            for k in post[i]:
                left[k] -= 1
                if not left[k]:
                    ready[k] = max(end[j] + (gap(k, j) if back else gap(j, k)) for j in pre[k])
        return end

    end = place(list(range(n)), False)
    best = end
    for turn in range(ROUNDS):
        late = [-x for x in place([-x for x in end], True)]
        end = min([place(late, False)] + [run(late, s, False) for s in SLACKS], key=max)
        if max(end) < max(best):
            best = end
        late = [-x for x in min([run([-x for x in end], s, True) for s in SLACKS], key=max)]
        end = min([place(late, False)] + [run(late, s, False) for s in SLACKS], key=max)
        if max(end) < max(best):
            best = end
    return [ops[i] for i in sorted(range(n), key=lambda i: (-1, i) if ops[i]["q"] and ops[i]["sem"] and not before[i] else (best[i] - ops[i]["busy"], best[i]))]


def emit(g, T, ops):
    eng = {"v": g.vector, "s": g.scalar, "t": g.tensor, "g": g, "y": g.sync}
    known = {q: {} for q in eng}
    pos = {q: 0 for q in eng}
    needed = set()
    for i, o in enumerate(ops):
        q = o["q"]
        if o["sem"] is None:
            o["src"], o["pos"] = q, pos[q]
            pos[q] += 1
        else:
            o["src"], o["pos"] = "d" + o["sem"], 0
        o["waits"], o["at"] = [], i
        if q is None:
            o["known"] = {}
            continue
        deps = {}
        for p in o["needs"]:
            if p["q"] == q == "t":
                continue
            if p["src"] not in deps or ops[deps[p["src"]]]["pos"] < p["pos"]:
                deps[p["src"]] = p["at"]
        for j in sorted(deps.values(), reverse=True):
            p = ops[j]
            if known[q].get(p["src"], -1) >= p["pos"]:
                continue
            o["waits"].append(j)
            needed.add(j)
            for s, n in p["known"].items():
                known[q][s] = max(known[q].get(s, -1), n)
            known[q][p["src"]] = max(known[q].get(p["src"], -1), p["pos"])
        o["known"] = dict(known[q])
    count = {q: 0 for q in eng}
    for i, o in enumerate(ops):
        q = o["q"]
        if o["sem"] is None and i in needed:
            count[q] += 1
            o["val"] = ("q" + q, count[q])
        elif o["sem"] is not None:
            o["val"] = (o["sem"], o["n"])
        if q is None:
            continue
        for j in o["waits"]:
            s, n = ops[j]["val"]
            eng[q].wait_ge(T.sem[s], n)
        r = o["fn"](eng[q])
        if o["sem"] is not None:
            for x in r:
                x.then_inc(T.sem[o["sem"]], 16)
        elif i in needed:
            r.then_inc(T.sem["q" + q], 1)


def rank_program(g, core, T, topo):
    rank = T.rank_of(core)
    if rank is None:
        return
    N = len(T.cores)
    nxt, prv = T.cores[(rank + 1) % N], T.cores[(rank - 1) % N]
    rid, pid = topo.addr(nxt, core)
    out_mask, n_out, n_in = topo.mask(core, nxt), len(topo.engines(core, nxt)), len(topo.engines(prv, core))
    ops = []
    sends, loaded = [0], [0.0]

    def op(q, fn, R=(), Wr=(), Xb=(), sem=None, n=0, busy=0.0, late=0.0, tag=None, rank=0):
        ops.append({"q": q, "fn": fn, "R": [tok(x) for x in R], "W": [tok(x) for x in Wr], "X": list(Xb), "sem": sem, "n": n,
                    "busy": busy, "late": late, "tag": tag, "rank": rank})

    def dmas(q, sem, pairs, R, Wr):
        op(q, lambda e: [e.dma_start(a, b) for a, b in pairs], R, Wr, sem=sem, n=16 * len(pairs),
           busy=ISSUE * len(pairs), late=1.6 + loaded[0] + sum(size(a) for a, b in pairs) / LOCAL)
        if not R:
            loaded[0] = ops[-1]["late"] - 1.6

    def send(dst, src, sem, R):
        sends[0] += n_out
        op("g", lambda e: e.remote_dma(dst, src, T.sem[sem], T.sem.sent, pid, rid, out_mask), R,
           busy=0.3, late=REMOTE, tag=(sem, size(src) / LINK))

    def arrive(sem, Wr):
        op(None, None, (), Wr, sem=sem, n=n_in)

    def vec(fn, o, R, Wr, Xb, rate=None):
        if rate is None:
            rate = 0.5 if all(width(tok(x)[0]) == 2 for x in list(R) + list(Wr)) else 1.0
        op("v", fn, R, Wr, Xb, busy=0.05 + count(o) * rate * CYCLE)

    def vmem(ap, val, Wr, Xb=()):
        vec(lambda e: e.memset(ap, val), ap, (), Wr, Xb, 0.5 if width(ap.name) == 2 else 1.0)

    def vcopy(o, i, R, Wr, Xb=(), rate=None):
        vec(lambda e: e.tensor_copy(o, i), o, R, Wr, Xb, rate)

    def vtt(o, a, b, alu, R, Wr, Xb=(), rate=None):
        vec(lambda e: e.tensor_tensor(o, a, b, alu), o, R, Wr, Xb, rate or (1.0 if Xb else 2.0))

    def vts(o, a, s1, s2, o0, o1, R, Wr, Xb=(), rate=None):
        if s2 is None:
            vec(lambda e: e.tensor_scalar(o, a, s1, None, o0), o, R, Wr, Xb, rate)
        else:
            vec(lambda e: e.tensor_scalar(o, a, s1, s2, o0, o1), o, R, Wr, Xb, rate)

    def vscan(o, a, b, init, o0, o1, R, Wr, Xb=()):
        vec(lambda e: e.tensor_tensor_scan(o, a, b, init, o0, o1), o, R, Wr, Xb)

    def act(o, i, R, Wr, Xb=(), fn=F.Copy, rate=1.0, first=False, later=False, **k):
        op("s", lambda e: e.activation(o, i, fn, **k), R, Wr, Xb, busy=0.065 + count(o) * rate * CYCLE, rank=later - first)

    def affine(q, o, i, scale, bias, R, Wr):
        if q == "v":
            vts(o, i, scale, bias, A.mult, A.add, R, Wr)
        else:
            act(o, i, R, Wr, fn=F.Identity, scale=scale, bias=bias)

    def mm(lst, R, Wr, Xb, first=False):
        def fn(e):
            r = None
            for a in lst:
                r = e.matmul(*a)
            return r
        cycles = sum(max(min(64, count(a[1])), count(a[2])) * (4 if width(a[1].name) == 4 else 1) for a in lst)
        op("t", fn, R, Wr, Xb, busy=cycles * PE_CYCLE, rank=-first)

    def iota(o, pat, base, cm, Wr):
        op("g", lambda e: e.iota(o, pat, base, cm, allow_small_or_imprecise_dtypes=True), (), Wr, busy=0.13 + 2 * count(o) * CYCLE)

    def sel(o, i, pat, cmp, base, cm, R, Wr):
        op("g", lambda e: e.affine_select(o, i, pat, cmp, 0.0, base, cm), R, Wr, busy=0.17 + 2 * count(o) * CYCLE)

    XB = {"X0": 5, "X1": 6, "X2": 7, "D": 4}

    for c in range(4):
        a, b = CUT0[c], CUT0[c + 1]
        dmas("ys"[c % 2], "sp%d" % c, [(T.Sb[:, BP + a:BP + b], T.sp[:, a:b])], (), [("Sb", 3 + a, 3 + b)])
    dmas("y", "itg", [(T.iti[:, :], T.itg[:, :])], (), ["iti"])
    dmas("s", "rot", [(T.roti[:, :], T.rot[:, :])], (), ["roti"])
    dmas("y", "hop", [(T.hpi[0:8, 0:3], T.hop[:, :])], (), ["hpi"])
    dmas("y", "rec", [(T.C2[:, k * WC:(k + 1) * WC], T.rec[:, :]) for k in range(2)], (), [("C2", 0, 2 * WC)])

    loaded[0] = 0.0

    vmem(T.of[:, :], 1.0, ["of"])
    vmem(T.Sb[:, 0:BP], 0.0, [("Sb", 0, 3)])
    vmem(T.Sb[:, BP + W:], 0.0, [("Sb", 3 + W, 4000)])
    vmem(T.nb[:, :], -float(BIG), ["nb"])
    vmem(T.ob[0:1, :], 8192.0, ["ob"])
    vmem(T.krow[0:1, :], 2048.0 * MAGIC / 8192, ["krow"])
    vmem(T.brow[0:1, :], 352.0 * BIG / 8192, ["brow"])
    vmem(T.itf[:, :, 0:290:289], 0.0, [("itf", a, a + 1) for a in (0, 289, 290, 579)])
    vmem(T.itf[:, :, 97:194:96], 0.0, [("itf", a, a + 1) for a in (97, 193, 387, 483)])
    vmem(T.I97[96:97, :], 1.0, [("I97", 1, 2)])
    vmem(T.Rw[:, :], 0.0, ["Rw"])
    vmem(T.Z[:, :], 0.0, ["Z"])
    vmem(T.V[:, 0:1], 0.0, [("V", 0, 1)])
    for u in range(2):
        vmem(T.G[:, 1568 * u:1568 * u + 16], 0.0, [("G", 10 + 2 * u, 11 + 2 * u)])
        vmem(T.G[:, 1568 * u + 1552:1568 * u + 1568], 0.0, [("G", 11 + 2 * u, 12 + 2 * u)])
    vmem(T.c17[:, :], float(2 ** 17), ["c17"])

    sel(T.Iw[:, 0:128], T.of[:, 0:128], [[1, 128]], A.is_equal, 0, -1, ["of"], [("Iw", 0, 1)])
    for nm, k in (("Db", 2.0), ("Jb", -1.0)):
        act(T[nm][:, :], T.Iw[:, 0:128], [("Iw", 0, 1)], [nm], scale=k)
    iota(T.crow[:, 0, :], [[0, 8], [-1, 64]], 16, 0, [("crow", 0, 1)])
    act(T.crow[0:1, 1, :], T.crow[0:1, 0, :], [("crow", 0, 1)], [("crow", 1, 2)], scale=-1.0)
    affine("s", T.LF[96:128, :], T.crow[96:128, 0, :], -8192.0, float(C0), [("crow", 0, 1)], [("LF", 1, 2)])
    affine("s", T.LB[96:128, :], T.crow[96:128, 0, :], 8192.0, float(C0 + 4096), [("crow", 0, 1)], [("LB", 1, 2)])
    vmem(T.crow[0:1, 0, 0:512:64], HUGE / 8192, [("crow", 0, 1)])
    vmem(T.crow[0:1, 1, 63:512:64], HUGE / 8192, [("crow", 1, 2)])
    sel(T.tm8[:, :], T.nb[:, :], [[-16, 8]], A.is_ge, 0, 1, ["nb"], ["tm8"])
    sel(T.ind[:, :], T.tm8[:, :], [[16, 8]], A.is_ge, 15, -1, ["tm8"], ["ind"])
    sel(T.Ew[0:8, :], T.of[0:8, :], [[1, 128]], A.is_ge, 0, -16, ["of"], ["Ew"])
    iota(T.g8[0:8, :], [[0, 2]], 0, -16, ["g8"])
    sel(T.Ew[0:8, :], T.Ew[0:8, :], [[-1, 128]], A.is_ge, 15, 16, ["Ew"], ["Ew"])
    iota(T.Lf[:, :], [[16, 2], [64, 8]], 0, 1, ["Lf"])
    iota(T.mp[:, :], [[16, 192]], 0, 1, ["mp"])
    act(T.I97[0:96, :], T.Iw[0:96, 0:96], [("Iw", 0, 1)], [("I97", 0, 1)])
    act(T.Iw[:, 128:240], T.Iw[:, 0:112], [("Iw", 0, 1)], [("Iw", 1, 2)])
    for k in range(2):
        act(T.Z[:, 15 + 128 * k:128 + 128 * k:16], T.ind[:, :], ["ind"], [("Z", k, k + 1)], scale=-1.0 / BIG)
    for S in ("S1", "S2"):
        vmem(T[S][:, 0:FP], 0.0, [(S, 0, 3)])
        vmem(T[S][:, FP + W:], 0.0, [(S, 3 + W, 4000)])

    def offsets(t):
        for u in range(2):
            vcopy(T.Lit[:, u, 96 * t:96 * t + 96], T.iti[:, 192 * t + u:192 * t + 192:2], ["iti"], [("Lit", 2 * t + u, 2 * t + u + 1)])

    def targets(t):
        for u in range(2):
            vcopy(T.itf[:, u, 1 + 96 * t:97 + 96 * t], T.iti[:, 192 * t + u:192 * t + 192:2], ["iti"], [("itf", 290 * u + 1 + 96 * t, 290 * u + 97 + 96 * t)])

    PIECES = [(1, -1), (0, 0), (1, 0), (0, 1)]

    def keys(t, d, B):
        lst = [(T[B][0:96, :, :], T.ob[0:1, 0:96], T.crow[0:1, d, :], True, False)]
        for j in range(d, d + 3):
            u, s = PIECES[j]
            a = 1 + 96 * t + s
            lst.append((T[B][0:96, :, 16 * j:16 * j + 16], T.itf[:, u, a:a + 96], T.Iw[:, 0:128], False, j == d + 2))
        mm(lst, ["ob", ("crow", d, d + 1), ("itf", 96 * t, 98 + 96 * t), ("itf", 290 + 96 * t, 388 + 96 * t), ("Iw", 0, 1)], [B], [XB[B]])

    def keys_out(d, B):
        K = "KB" if d else "KF"
        act(T[K][0:96, :], T[B][0:96, :, :], [B], [K], [XB[B]])

    def rows(t, to, B):
        act(T.Rhi[:, :], T.Qf[:, :], ["Qf"], ["Rhi"])
        mm([(T[B][:, 0:192], T.Iw[:, 0:128], T.Qf[:, :], True, False), (T[B][:, 0:192], T.Jb[:, :], T.Rhi[:, :], False, True)],
           ["Rhi", "Qf", "Jb", ("Iw", 0, 1)], [B], [XB[B]])
        act(T.Rlo[:, :], T[B][:, 0:192], [B], ["Rlo"], [XB[B]])
        affine("s", T.b2[:, :], T.Qf[:, :], 2.0 ** -11, MAGIC, ["Qf"], ["b2"])
        affine("s", T.Rk[:, :], T.b2[:, :], -2048.0, 2048.0 * MAGIC, ["b2"], ["Rk"])
        dmas("y", "rw%s" % t, [(T[to][4 * j:128:16, :], T[nm][:, :]) for j, nm in enumerate(("Rhi", "Rk", "Rlo"))], ["Rhi", "Rlo", "Rk"], [to])
        ops[-1]["late"] = ROWS

    def window(which):
        for r in which:
            if r < WG:
                sel(T.Rw[:, r:W:16], T.Rr[:, 192 * r:192 * r + 192], [[0, 192]], A.is_ge, 0, 0, ["Rr"], [("Rw", r, r + 1)])
            else:
                act(T.Rw[:, r:W:16], T.Rr[:, 192 * r:192 * r + 192], ["Rr", ("G", 3, 4)], [("Rw", r, r + 1)], later=True)

    banks = [0]

    def votes(S, ja, jb, mode, closed=False):
        b16 = S == "Sb"
        base = (BP if b16 else FP) - 3
        M2, M4, M7 = ("N2", "N4", "N7") if b16 else ("M2", "M4", "M7")
        I, J, D2 = ("Ib", "Jb", "Db") if b16 else ("Iw", "Jf", "Df")
        first = ja in (0, X + 3) if not b16 else ja == 0
        a2, a4, an = (ja, ja, max(ja, 1)) if first else (ja - 1, ja - 3, ja - 6)
        b2, b4, bn = (jb, jb, jb) if closed else (jb - 1, jb - 3, jb - 6)

        def m2():
            vscan(T[M2][:, a2:b2], T[S][:, base + a2:base + b2], T[S][:, base + a2 + 1:base + b2 + 1], HUGE, A.min, A.max, [(S, a2, b2 + 1)], [(M2, a2, b2)])

        def m4():
            vscan(T[M4][:, a4:b4], T[M2][:, a4:b4], T[M2][:, a4 + 2:b4 + 2], HUGE, A.min, A.max, [(M2, a4, b4 + 2)], [(M4, a4, b4)])

        def m7(a, b):
            vscan(T[M7][:, a:b], T[M4][:, a:b], T[M4][:, a + 3:b + 3], HUGE, A.min, A.max, [(M4, a, b + 3)], [(M7, a, b)])

        def diff(a, b):
            vscan(T.V[:, a:b], T[S][:, base + 3 + a:base + 3 + b], T[M7][:, a:b], 0.0, A.max, A.subtract, [(S, a + 3, b + 3), (M7, a, b)], [("V", a, b)])

        def tensor(a, b, md):
            k = banks[0] % 4
            banks[0] += 1
            P = ("PA", "PB")[k // 2]
            d = T[P][:, 512 * (k % 2):512 * (k % 2) + b - a]
            s = T[S][:, base + 3 + a:base + 3 + b]
            bank = (P, k % 2, k % 2 + 1)
            mm([(d, T[D2 if md == 2 else I][:, 0:128], s, True, False)], [D2 if md == 2 else I, (S, a + 3, b + 3)], [bank], [k])
            if md == 2:
                mm([(d, T[J][:, :], T[M4][:, a:b], False, False)], [J, (M4, a, b)], [bank], [k])
                mm([(d, T[J][:, :], T[M4][:, a + 3:b + 3], False, True)], [J, (M4, a + 3, b + 3)], [bank], [k])
            else:
                mm([(d, T[J][:, :], T[M7][:, a:b], False, True)], [J, (M7, a, b)], [bank], [k])
            act(T.V[:, a:b], d, [bank], [("V", a, b)], [k], later=not b16)

        def rest():
            md, cols = mode
            mid = min(an + cols, bn)
            if mid < bn:
                m7(mid, bn)
                diff(mid, bn)

        def out():
            md, cols = mode
            mid = min(an + cols, bn)
            if md == 3 and mid > an:
                m7(an, mid)
            n = (mid - an + CHUNK - 1) // CHUNK
            for i in range(n):
                tensor(an + (mid - an) * i // n, an + (mid - an) * (i + 1) // n, md)
        return m2, m4, rest, out

    def votes32(S, ja, jb, na, on_tensor):
        base, nb, hb = FP - 3, min(jb - 6, X + 9 if ja < X else W), X + 9 if ja < X + 9 < jb else jb
        pre = T.PA[:, 512 + na + 6 - ja:512 + nb + 6 - ja]
        vscan(T.H[:, hb - 1:ja - 1 if ja else None:-1], T.PA[:, 0:hb - ja], T[S][:, base + hb - 1:base + ja - 1:-1], 0.0, A.mult, A.max,
              ["msk", (S, ja, hb)], [("H", ja, hb)], [0])
        vscan(T.PA[:, 512:512 + jb - ja], T.PA[:, 0:jb - ja], T[S][:, base + ja:base + jb], 0.0, A.mult, A.max, ["msk", (S, ja, jb)], [("PA", 1, 2)], [0, 1])
        s = T[S][:, base + 3 + na:base + 3 + nb]
        if not on_tensor:
            vtt(pre, T.H[:, na:nb], pre, A.max, [("H", na, nb), ("PA", 1, 2)], [("PA", 1, 2)], [1])
            vtt(T.V[:, na:nb], s, pre, A.subtract, [(S, na + 3, nb + 3), ("PA", 1, 2)], [("V", na, nb)], [1])
            return
        vtt(T.M[:, na:nb], T.H[:, na:nb], pre, A.max, [("H", na, nb), ("PA", 1, 2)], [("M", na, nb)], [1])
        k = banks[0] % 2
        banks[0] += 1
        d = T.PB[:, 512 * k:512 * k + nb - na]
        mm([(d, T.Iw[:, 0:128], s, True, False)], [("Iw", 0, 1), (S, na + 3, nb + 3)], [("PB", k, k + 1)], [2 + k])
        mm([(d, T.Jf[:, :], T.M[:, na:nb], False, True)], ["Jf", ("M", na, nb)], [("PB", k, k + 1)], [2 + k])
        act(T.V[:, na:nb], d, [("PB", k, k + 1)], [("V", na, nb)], [2 + k])

    v0 = [votes("Sb", (CUT0[c] + 3) * (c > 0), CUT0[c + 1] + (3 if c < 3 else 6), MODE0[c]) for c in range(4)]
    for v in v0[:3]:
        for k in (0, 1, 3, 2):
            v[k]()
    vcopy(T.Qf[:, :], T.roti[:, :], ["roti"], ["Qf"])
    rows("", "Rw", "X1")
    v0[3][0](); v0[3][1](); v0[3][3]()
    targets(0); keys(0, 0, "X2")
    offsets(0)
    v0[3][2](); keys_out(0, "X2"); keys(0, 1, "X2")

    for t in range(FR):
        last = t == FR - 1
        So = ("Sb", "S1", "S2")[t]
        Sn = ("S1", "S2", "S1")[t]
        so = BP if t == 0 else FP
        Tl = "T0" if t == 0 else "T1"
        Tt = ("T0", "T1", "T2")[t]
        Ts, Qu = "Ts%d" % t, "Qu%d" % t
        turn = -16 * t % 128
        table, tk = T.C2[:, :], "C2"

        mm([(T.D[0:96, :], T.ob[0:1, 0:96], T.brow[0:1, :], True, False)], ["ob", "brow"], ["D"], [4])
        for u in range(2):
            for h, q in enumerate("vs"):
                o = T.G[:, 1568 * u + 16 + 768 * h:1568 * u + 16 + 768 * h + 768]
                w = T.V[:, :].indirect(T.Lit[:, u, 96 * t + 48 * h:96 * t + 48 * h + 48])
                R, Wr = ["V", ("Lit", 2 * t + u, 2 * t + u + 1)], [("G", 2 * u + h, 2 * u + h + 1)]
                if q == "v":
                    vts(o, w, 0.0, 64.0, A.is_ge, A.mult, R, Wr, rate=GATHER)
                else:
                    act(o, w, R, Wr, fn=F.Relu, rate=GATHER, bias=64.0, scale=2.0 ** 38)
            lst = []
            for j, (uu, s) in enumerate(PIECES):
                if uu == u:
                    for r in range(16):
                        a = 1568 * u + 16 * (1 + s) + r
                        lst.append((T.D[0:96, 16 * j + r:512:64], T.G[:, a:a + 16 * 95 + 1:16], T.ind[:, :], False, u == 1 and j == 2 and r == 15))
            mm(lst, [("G", 2 * u, 2 * u + 2), ("G", 10, 14), "ind"], ["D"], [4])
        if t == 0:
            keys_out(1, "X2")
            vcopy(T.hpf[0:8, 0:3], T.hpi[0:8, 0:3], ["hpi"], ["hpf"])
            act(T.C2[:, 2 * WC:], T.C2[:, 0:16], [("C2", 0, 16)], [("C2", 2 * WC, 2 * WC + 16)])
            mm([(T.X0[:, 0:3], T.Ew[0:8, 0:128], T.hpf[0:8, 0:3], True, True),
                (T.X0[:, 3:5], T.Ew[0:8, 0:128], T.g8[0:8, :], True, True)], ["Ew", "hpf", "g8"], ["X0"], [5])
            act(T.hv[:, 0:5], T.X0[:, 0:5], ["X0"], [("hv", 0, 5)], [5])
            vts(T.Lm[:, :], T.Lf[:, :], T.hv[:, 3:4], None, A.add, None, ["Lf", ("hv", 0, 5)], ["Lm"])
        else:
            window(range(WG, 16))
            if not last:
                offsets(t + 1)
        if not last:
            targets(t + 1)
        vscan(T.LF[0:96, 0:496], T.D[0:96, 0:496], T.KF[0:96, 0:496], HUGE, A.min, A.max, ["D", "KF"], [("LF", 0, 1)], [4])
        vscan(T.LB[0:96, 511:15:-1], T.D[0:96, 511:15:-1], T.KB[0:96, 511:15:-1], HUGE, A.min, A.max, ["D", "KB"], [("LB", 0, 1)], [4])
        for L, M, B in (("LF", "MF", "X0"), ("LB", "MB", "X1")):
            for u in range(2):
                (vcopy if L == "LF" and u < MV else act)(T[M][:, u, :], T[L][:, 16:496].indirect(T.Lm[:, 8 * u:8 * u + 8]), [L, "Lm"], [(M, u, u + 1)], rate=GATHER)
                mm([(T[B][:, u:192:2], T[M][0:97, u, :], T.I97[0:97, :], True, True)], [(M, u, u + 1), "I97"], [B], [XB[B]])
        if t == 0:
            act(T.hv[:, 5:8], T.hv[:, 0:3], [("hv", 0, 5)], [("hv", 5, 8)], scale=2.0 ** -11)
            act(T.mc[:, :], T.mp[:, :], ["mp", ("hv", 0, 5)], ["mc"], fn=F.Identity, bias=T.hv[:, 3:4])
            for c in range(4):
                act(T.Rr[:, X * c:X * c + X], T.G[:, 0:X], ["G"], [("Rr", c, c + 1)], scale=0.0, later=True)
            act(T.Jf[:, :], T.Iw[:, 0:128], [("Iw", 0, 1)], ["Jf"], scale=-1.0)
            act(T.Kw[:, :], T.Iw[:, :], ["Iw"], ["Kw"], scale=-2048.0)
            act(T.Df[:, :], T.Iw[:, 0:128], [("Iw", 0, 1)], ["Df"], scale=2.0)
        act(T.Hd[:, t, 0:128 + turn], T.Iw[:, 0:128 + turn], ["Iw", ("hv", 0, 5)], [("Hd", t, t + 1)], fn=F.Identity, scale=T.hv[:, t:t + 1])
        if not last:
            keys(t + 1, 0, "X2")
        vscan(T.PA[:, 704:896], T.c17[:, :], T.X0[:, 0:192], HUGE, A.add, A.min, ["c17", "X0"], [("PA", 1, 2)], [1, 5])
        if t == 0 and not PAIRS:
            vmem(T.PA[:, 0:511], 1.0, [("PA", 0, 1), "msk"], [0])
            vmem(T.PA[:, 0:511:7], 0.0, [("PA", 0, 1), "msk"], [0])
        if t == 0:
            offsets(1)
        vscan(T.B2[:, ::-1], T.c17[:, :], T.X1[:, 191::-1], HUGE, A.add, A.min, ["c17", "X1"], ["B2"], [6])

        def sources(parts):
            steps = []
            for k, (a, b) in enumerate(parts):
                c = slice(a, b)
                F2, sd, sg = T.PA[:, 704 + a:704 + b], T.PA[:, 512 + a:512 + b], T.PB[:, 512 * k + a:512 * k + b]
                pa = ("sd", a, b)
                steps.append([
                    lambda c=c, F2=F2, a=a, b=b: vtt(T.Dd[:, c], T.B2[:, c], F2, A.subtract, ["B2", ("PA", 1, 2)], [("Dd", a, b)], [1]),
                    lambda c=c, F2=F2, a=a, b=b: vtt(T.Wi[:, c], T.B2[:, c], F2, A.min, ["B2", ("PA", 1, 2)], [("Wi", a, b)], [1]),
                    lambda c=c, sg=sg, a=a, b=b, k=k: act(sg, T.Dd[:, c], [("Dd", a, b)], [("PB", k, k + 1)], [2 + k], fn=F.Sign),
                    lambda c=c, a=a, b=b: vts(T.di[:, c], T.Wi[:, c], 2.0 ** -13, -C0 / 8192 - 0.4375, A.mult, A.add, [("Wi", a, b)], [("di", a, b)]),
                    lambda c=c, a=a, b=b: vts(T.pi[:, c], T.Wi[:, c], 4095, None, A.bitwise_and, None, [("Wi", a, b)], [("pi", a, b)]),
                    lambda c=c, sd=sd, sg=sg, a=a, b=b, k=k, pa=pa: vtt(sd, T.di[:, c], sg, A.mult, [("di", a, b), ("PB", k, k + 1), ("PA", 1, 2)], [pa], [2 + k, 1]),
                    lambda c=c, sd=sd, a=a, b=b, pa=pa: vtt(sd, T.pi[:, c], sd, A.add, [("pi", a, b), pa, ("PA", 1, 2)], [pa], [1]),
                    lambda c=c, sd=sd, a=a, b=b, pa=pa: vts(T.Ls[:, c], sd, 0.0, float(W - 1), A.max, A.min, [pa, ("PA", 1, 2)], [("Ls", a, b)], [1], rate=1.0),
                    lambda c=c, sd=sd, a=a, b=b, pa=pa: vtt(T.dm[:, c], T.mc[:, c], sd, A.subtract, ["mc", pa, ("PA", 1, 2)], [("dm", a, b)], [1]),
                    lambda c=c, a=a, b=b: affine(EQ[last], T.a2[:, c], T.dm[:, c], T.hv[:, 5 + t:6 + t], MAGIC, [("dm", a, b), ("hv", 5, 8)], [("a2", a, b)])])
            return steps

        def gb(c):
            a, b = c
            act(T.Rg[:, 16 * a:16 * b], T.Rw[:, :].indirect(T.Ls[:, a:b]), ["Rw", ("Ls", a, b)], [("Rg", a, b)], rate=GATHER)

        def gc(c, q, small=0):
            a, b = c
            w, R = T[So][:, so:so + W].indirect(T.Ls[:, a:b]), [So, ("Ls", a, b)]
            if a >= 144:
                o, Wr = T[Ts][:, 16 * a - 2304:16 * b - 2304], [(Ts, a, b)]
            else:
                o, Wr = T[Tl][:, X + 16 * a:X + 16 * b], [(Tl, X + 16 * a, X + 16 * b)]
            k = 2.0 ** -10 if small else 1.0
            if q == "v":
                vts(o, w, k, None, A.mult, None, R, Wr, rate=GATHER)
            else:
                act(o, w, R, Wr, rate=GATHER, scale=k)

        def ext(c, B):
            a, b = c
            o = turn if a >= 144 else 0
            mm([(T[B][:, 0:b - a], T.Kw[:, o:o + 128], T.a2[:, a:b], True, False), (T[B][:, 0:b - a], T.ob[0:1, :], T.krow[0:1, 0:b - a], False, False),
                (T[B][:, 0:b - a], T.Hd[:, t, o:o + 128], T.dm[:, a:b], False, False)],
               ["Kw", "ob", "krow", ("Hd", t, t + 1), ("dm", a, b), ("a2", a, b)], [B], [XB[B]])
            lst = [(T[B][:, 0:b - a], T.Z[:, 15 - r + o:143 - r + o], T.Rg[:, 16 * a + r:16 * b:16], False, r == 15) for r in range(16)]
            mm(lst, ["Z", ("Rg", a, b)], [B], [XB[B]])

        def qq(c, B):
            a, b = c
            if a >= 144:
                vts(T.Qs[:, 48 * t:48 * t + 48], T[B][:, 0:48], float(WC), None, A.add, None, [B], [("Qs", t, t + 1)], [XB[B]])
                send(T[Qu][:, 0:48], T.Qs[:, 48 * t:48 * t + 48], "aQ%d" % t, [("Qs", t, t + 1)])
            else:
                vts(T[Qu][:, 48 + a:48 + b], T[B][:, 0:b - a], float(WC), None, A.add, None, [B], [(Qu, 48 + a, 48 + b)], [XB[B]])

        def gd(a, b, small=0):
            src, nm = (T[Tt][:, a:b], Tt) if a < X else (T[Tl][:, a:b], Tl)
            w, R = table.indirect(T[Qu][:, a // 16:b // 16]), [tk, (Qu, a // 16, b // 16)]
            if small:
                act(T.Cg[:, a:b], w, R, [("Cg", a, b)], rate=GATHER, scale=1024.0)
                B = "X1" if b == X else "X0"
                mm([(T[B][:, 0:b - a], T.Iw[:, turn:turn + 128], T[Tt][:, a:b], True, True)], ["Iw", (Tt, a, b)], [B], [XB[B]])
                vscan(T[Sn][:, FP + a:FP + b], T.Cg[:, a:b], T[B][:, 0:b - a], 0.0, A.max, A.mult, [("Cg", a, b), B], [(Sn, 3 + a, 3 + b)], [XB[B]])
            else:
                vtt(T[Sn][:, FP + a:FP + b], w, src, A.mult, R + [(nm, a, b)], [(Sn, 3 + a, 3 + b)], rate=GATHER)

        def pass_on(a, b, i, q, small=0):
            c = (144 + a // 16, 144 + b // 16)
            gc(c, q, small)
            send(T[Tt][:, a:b], T[Ts][:, a:b], "aT%d%d" % (t, i), [(Ts,) + c])
            arrive("aT%d%d" % (t, i), [(Tt, a, b)])

        top = (144, 192)
        arrive("aQ%d" % t, [(Qu, 0, 48)])
        if not last:
            cs = list(zip(CUT[:-1], CUT[1:]))
            n = [X + 16 * k for k in CUT]
            if PAIRS:
                va = [votes(Sn, n[i] + 3, n[i + 1] + (3 if i + 1 < len(cs) else 6), PMODE[i]) for i in range(len(cs))]
                va += [votes(Sn, 0, X + 3, PMODE[-1], True)] if PAIRS == 1 else [votes(Sn, 0, 390, PMODE[-1]), votes(Sn, 390, X + 3, PMODE[-1], True)]
            done = [X + 9, 0]

            def vote_to(j, start):
                parts = (j - done[0] + SPAN - 1) // SPAN
                for k in range(parts):
                    a = done[0]
                    b = a + (j - a) // 7 // (parts - k) * 7
                    votes32(Sn, a, b, max(a - 6, start), MODE[done[1]] == "t")
                    done[:] = [b, done[1] + 1]

            for fs in zip(*sources([(0, HEAD), (HEAD, 192)] if HEAD else [(0, 192)])):
                for f in fs:
                    f()
            keys_out(0, "X2"); keys(t + 1, 1, "X2")
            gb(cs[0])
            for i, c in enumerate(cs):
                if i:
                    gb(c)
                ext(c, "X%d" % (i % 2)); gc(c, GC[i])
                if i == TOP_T:
                    for k in range(t + 1):
                        pass_on(X * k // (t + 1), X * (k + 1) // (t + 1), k, GC[-1], t)
                qq(c, "X%d" % (i % 2))
                if i == TOP_Q:
                    gb(top); ext(top, "D"); qq(top, "D")
                if i + 1 == len(cs):
                    vcopy(T.Qf[:, :], T[Qu][:, :], [Qu], ["Qf"])
                    rows(t, "Rr", "D")
                gd(n[i], n[i + 1])
                if PAIRS:
                    va[i][0](); va[i][1]()
                else:
                    vote_to((n[i + 1] + 3) // 7 * 7 if i + 1 < len(cs) else 3080, X + 9)
            keys_out(1, "X2")
            done[0] = 0
            if PAIRS:
                for k in range(t + 1):
                    gd(X * k // (t + 1), X * (k + 1) // (t + 1), t)
                for v in va[:len(cs)]:
                    v[3](); v[2]()
                for k in (0, 1, 3, 2):
                    for v in va[len(cs):]:
                        v[k]()
            else:
                for k in range(2):
                    gd(X // 2 * k, X // 2 * (k + 1), t)
                    vote_to((385, X + 16)[k], 1)
            window(range(WG))
        else:
            acc = T.PB

            def fold(parts, start, stop):
                lst = []
                for i, (a, b) in enumerate(parts):
                    lst.append((acc[:, a % 512:a % 512 + b - a], T.Iw[:, 0:128], T[Sn][:, FP + a:FP + b], start and i == 0, stop and i == len(parts) - 1))
                mm(lst, ["Iw"] + [(Sn, 3 + a, 3 + b) for a, b in parts], ["acc", ("PB", 0, 1)], [2])

            def store(h):
                a, b = 256 * h, 256 * h + 256
                vtt(T.Y[:, a:b], T[Sn][:, FP + a:FP + b], acc[:, a:b], A.add, [(Sn, 3 + a, 3 + b), ("acc", a, b)], [("Y", h, h + 1)], [2])
                dmas("ys"[h], "y%d" % h, [(T.y[:, a:b], T.Y[:, a:b])], [("Y", h, h + 1)], [("out", h, h + 1)])

            c0, c1, c2 = zip(CUTL[:-1], CUTL[1:])
            for fs in zip(*sources([(144, 192), (0, 144)] if HEAD else [(0, 192)])):
                for f in fs:
                    f()

            def add(a, b):
                o = acc[:, a % 512:a % 512 + b - a]
                vtt(o, T[Sn][:, FP + a:FP + b], o, A.add, [(Sn, 3 + a, 3 + b)], [("acc", a % 512, a % 512 + b - a)], [2])

            pass_on(256, X, 0, "v", 1); gb(top); pass_on(0, 256, 1, "v", 1)
            ext(top, "D"); gb(c0); gc(c0, "v"); qq(top, "D"); ext(c0, "X1")
            gb(c1); gc((48, K3), "v")
            ext(c1, "X0"); qq(c0, "X1"); gd(1024, 2 * X); fold([(1024, 1536)], True, False); gd(X, 1024)
            gb(c2); ext(c2, "X1"); gc((K3, 144), "s")
            fold([(768, 1024)], False, FOLD == 0)
            qq(c1, "X0"); gd(2 * X, 3 * X)
            for k, (a, b) in enumerate(((1536, 2048), (2048, 2304))):
                if k < FOLD:
                    fold([(a, b)], False, k + 1 == FOLD)
                else:
                    add(a, b)
            qq(c2, "X1"); gd(3 * X, W); add(3 * X, 2560); add(2560, 2816); add(2816, W)
            gd(256, X, 1); store(1); gd(0, 256, 1); add(512, X); store(0)
    op("g", lambda e: e.wait_ge(T.sem.sent, sends[0]), ["out"])
    emit(g, T, arrange(ops))
